import numpy as np
import ml_dtypes


def mxq(x, axis, fmt="e4m3"):
    dtype, down = {"e4m3": (ml_dtypes.float8_e4m3fn, 7), "e5m2": (ml_dtypes.float8_e5m2, 14)}[fmt]
    v = np.moveaxis(np.asarray(x, np.float32).astype(ml_dtypes.bfloat16).astype(np.float64), axis, -1)
    blocks = v.reshape(v.shape[:-1] + (-1, 32))
    amax = np.abs(blocks).max(-1, keepdims=True)
    byte = np.maximum(np.where(amax > 0, np.frexp(amax)[1] - 1 + 127, 0) - down, 1)
    scale = np.exp2(byte - 127.0)
    codes = (blocks / scale).astype(np.float32).astype(dtype).astype(np.float64)
    return np.moveaxis((codes * scale).reshape(v.shape), -1, axis)


WIDE = False


def mx_kscale(k):
    if not WIDE:
        return np.ones(k)
    levels = np.array([10, -10, 5, -5, 0])
    if k % 512:
        return np.exp2(np.random.permutation(np.resize(levels, k // 32))).repeat(32)
    a = np.empty((k // 512, 16))
    for p in range(k // 512):
        a[p, :8] = np.random.permutation(np.resize(levels, 8))
        for g in range(8):
            far = levels[np.abs(levels - a[p, g]) >= 10]
            a[p, g + 8] = far[np.random.randint(len(far))]
    return np.exp2(a.ravel()).repeat(32)


def f64(x):
    return np.asarray(x).astype(np.float64)


def striped(idx):
    return np.tile(idx.reshape(-1, 16).T, (8, 1)).astype(np.uint16)


def unstriped(offs):
    return offs[:16].T.reshape(-1).astype(np.int64)


K, T, S, V, N = 512, 1024, 512, 256, 128
P = 2 ** 7


def setup_inputs():
    n = np.random.standard_normal
    s = mx_kscale(K)[:, None]
    return {
        "xT": (n((K, T)) * s).astype(np.float32),
        "w1": (n((K, N)) / np.sqrt(K) / s).astype(np.float32),
        "bound": np.tile(np.random.uniform(0.3, 1.2, V), (P, 1)).astype(np.float32),
        "offs": striped(np.random.permutation(T)[:S]),
        "cen": striped(np.random.permutation(S)[:V]),
        "pos1": striped(np.random.permutation(S)[:V]),
        "pos2": striped(np.random.permutation(S)[:V]),
    }


def reference(xT, w1, bound, offs, cen, pos1, pos2):
    xq = mxq(f64(xT)[:, unstriped(offs)], 0, "e4m3")
    y = mxq(f64(w1), 0, "e4m3").T @ xq
    yc = y[:, unstriped(cen)]
    low = -1.0 * f64(bound)[:1]
    return yc + (np.maximum(np.minimum(y[:, unstriped(pos1)] - yc, f64(bound)[:1]), low) + np.maximum(np.minimum(y[:, unstriped(pos2)] - yc, f64(bound)[:1]), low)) / 2

@@ -1,0 +1,127 @@
+from contextlib import ExitStack
+
+import concourse.mybir as mybir
+
+K, T, S, V, N = 512, 1024, 512, 256, 128
+FLOPS = 2 * K * N * S
+
+F32 = mybir.dt.float32
+BF16 = mybir.dt.bfloat16
+U32 = mybir.dt.uint32
+U16 = mybir.dt.uint16
+U8 = mybir.dt.uint8
+FP8X4 = mybir.dt.float8_e4m3fn_x4
+ALU = mybir.AluOpType
+
+P = 128
+PACK = 4
+PIECE = 128
+PIECES = S // PIECE
+HALF = S // 2
+PER_COL = 16
+
+
+def tile_picked_huber_none_e_kernel(tc, xT, w1, bound, offs, cen, pos1, pos2, out):
+    nc = tc.nc
+    with ExitStack() as ctx:
+        lists = ctx.enter_context(tc.tile_pool(name="lists", bufs=1))
+        sb = ctx.enter_context(tc.tile_pool(name="sb", bufs=1))
+        ps = ctx.enter_context(tc.psum_pool(name="ps", bufs=1))
+
+        offs_t = lists.tile([P, S // PER_COL], U16, name="offs_t")
+        cen_t = lists.tile([P, V // PER_COL], U16, name="cen_t")
+        pos1_t = lists.tile([P, V // PER_COL], U16, name="pos1_t")
+        pos2_t = lists.tile([P, V // PER_COL], U16, name="pos2_t")
+
+        x_rows = xT.rearrange("(p j) t -> p j t", j=PACK)
+        plane = [sb.tile([P, T], F32, name=f"plane{j}") for j in range(PACK)]
+        w_raw = sb.tile([P, PACK, N], F32, name="w_raw")
+        b_t = sb.tile([P, V], F32, name="b_t")
+
+        nc.sync.dma_start(plane[0][:], x_rows[:, 0, :])
+        nc.sync.dma_start(offs_t[:], offs)
+        nc.sync.dma_start(w_raw[:], w1.rearrange("(p j) m -> p j m", j=PACK))
+        for j in range(1, PACK):
+            nc.sync.dma_start(plane[j][:], x_rows[:, j, :])
+        nc.sync.dma_start(cen_t[:], cen)
+        nc.sync.dma_start(pos1_t[:], pos1)
+        nc.sync.dma_start(pos2_t[:], pos2)
+        nc.sync.dma_start(b_t[:], bound)
+
+        def entries(first, count):
+            return offs_t[:, first // PER_COL : (first + count) // PER_COL]
+
+        low = [sb.tile([P, 2, HALF], F32, name=f"low{h}") for h in range(2)]
+        high = [sb.tile([P, 2, PIECE], F32, name=f"high{s}") for s in range(PIECES)]
+        woven = [sb.tile([P, PIECE, PACK], BF16, name=f"woven{s}", align_bytes=64) for s in range(PIECES)]
+
+        w_woven = sb.tile([P, N, PACK], BF16, name="w_woven", align_bytes=64)
+        w_codes = sb.tile([P, N], U32, name="w_codes", align_bytes=64)
+        w_scales = sb.tile([P, N], U8, name="w_scales", align_bytes=64)
+        nc.scalar.copy(w_woven[:], w_raw[:].rearrange("p j m -> p m j"))
+        nc.vector.quantize_mx(out=w_codes[:].bitcast(FP8X4), scales=w_scales[:], in_=w_woven[:].rearrange("p m j -> p (m j)"))
+
+        for j in range(2):
+            for h in range(2):
+                nc.vector.tensor_copy(low[h][:, j, :], plane[j][:].indirect(entries(h * HALF, HALF)))
+        for s in range(PIECES):
+            h, first = divmod(s * PIECE, HALF)
+            nc.scalar.copy(woven[s][:, :, 0:2], low[h][:, :, first : first + PIECE].rearrange("p j n -> p n j"))
+        for j in range(2):
+            for s in range(PIECES):
+                nc.vector.tensor_copy(high[s][:, j, :], plane[2 + j][:].indirect(entries(s * PIECE, PIECE)))
+
+        for s in range(PIECES):
+            pairs = high[s][:].rearrange("p j n -> p n j")
+            if s == PIECES - 1:
+                nc.vector.tensor_copy(woven[s][:, :, 2:4], pairs)
+            else:
+                nc.scalar.copy(woven[s][:, :, 2:4], pairs)
+
+        y = sb.tile([P, S], F32, name="y")
+        order = [0, 1, 3, 2]
+        for s in order:
+            codes = sb.tile([P, PIECE], U32, name=f"codes{s}", align_bytes=64)
+            scales = sb.tile([P, PIECE], U8, name=f"scales{s}", align_bytes=64)
+            nc.vector.quantize_mx(out=codes[:].bitcast(FP8X4), scales=scales[:], in_=woven[s][:].rearrange("p n j -> p (n j)"))
+            acc = ps.tile([P, PIECE], F32, name=f"acc{s}")
+            nc.tensor.matmul_mx(
+                out=acc[:],
+                lhsT=w_codes[:].bitcast(FP8X4),
+                lhsT_scale=w_scales[:],
+                rhs=codes[:].bitcast(FP8X4),
+                rhs_scale=scales[:],
+                start=True,
+                stop=True,
+            )
+            if s == order[-1]:
+                nc.vector.tensor_copy(y[:, s * PIECE : (s + 1) * PIECE], acc[:])
+            else:
+                nc.scalar.copy(y[:, s * PIECE : (s + 1) * PIECE], acc[:])
+
+        b_half = sb.tile([P, V], F32, name="b_half")
+        nc.vector.tensor_scalar(b_half[:], b_t[:], 0.5, None, ALU.mult)
+
+        centre = sb.tile([P, V], F32, name="centre")
+        near = [sb.tile([P, V], F32, name=f"near{d}") for d in range(2)]
+        upper = sb.tile([P, V], F32, name="upper")
+        lower_half = sb.tile([P, V], F32, name="lower_half")
+        nc.vector.tensor_copy(centre[:], y[:].indirect(cen_t[:]))
+        nc.vector.tensor_copy(near[0][:], y[:].indirect(pos1_t[:]))
+        nc.vector.tensor_tensor(upper[:], centre[:], b_t[:], ALU.add)
+        nc.vector.tensor_copy(near[1][:], y[:].indirect(pos2_t[:]))
+        nc.vector.scalar_tensor_tensor(lower_half[:], centre[:], 0.5, b_half[:], ALU.mult, ALU.subtract)
+        capped = [sb.tile([P, V], F32, name=f"capped{d}") for d in range(2)]
+        for d in range(2):
+            nc.vector.tensor_tensor(capped[d][:], near[d][:], upper[:], ALU.min)
+        first_half = sb.tile([P, V], F32, name="first_half")
+        nc.vector.scalar_tensor_tensor(first_half[:], capped[0][:], 0.5, lower_half[:], ALU.mult, ALU.max)
+        cols = [slice(0, V // 2), slice(V // 2, V)]
+        second_half = [sb.tile([P, V // 2], F32, name=f"second_half{h}") for h in range(2)]
+        for h in range(2):
+            nc.vector.scalar_tensor_tensor(second_half[h][:], capped[1][:, cols[h]], 0.5, lower_half[:, cols[h]], ALU.mult, ALU.max)
+        queues = [nc.scalar, nc.sync]
+        for h in range(2):
+            result = sb.tile([P, V // 2], F32, name=f"result{h}")
+            nc.vector.tensor_tensor(result[:], first_half[:, cols[h]], second_half[h][:], ALU.add)
+            queues[h].dma_start(out[:, cols[h]], result[:])

@@ -52,7 +52,7 @@ def tile_picked_huber_none_e_kernel(tc, xT, w1, bound, offs, cen, pos1, pos2, ou
             return offs_t[:, first // PER_COL : (first + count) // PER_COL]
 
         low = [sb.tile([P, 2, HALF], F32, name=f"low{h}") for h in range(2)]
-        high = [sb.tile([P, 2, PIECE], F32, name=f"high{s}") for s in range(PIECES)]
+        high = [sb.tile([P, 2, PIECE], F32, name=f"high{s}") for s in range(PIECES - 1)]
         woven = [sb.tile([P, PIECE, PACK], BF16, name=f"woven{s}", align_bytes=64) for s in range(PIECES)]
 
         w_woven = sb.tile([P, N, PACK], BF16, name="w_woven", align_bytes=64)
@@ -69,14 +69,11 @@ def tile_picked_huber_none_e_kernel(tc, xT, w1, bound, offs, cen, pos1, pos2, ou
             nc.scalar.copy(woven[s][:, :, 0:2], low[h][:, :, first : first + PIECE].rearrange("p j n -> p n j"))
         for j in range(2):
             for s in range(PIECES):
-                nc.vector.tensor_copy(high[s][:, j, :], plane[2 + j][:].indirect(entries(s * PIECE, PIECE)))
+                target = woven[s][:, :, 2 + j] if s == PIECES - 1 else high[s][:, j, :]
+                nc.vector.tensor_copy(target, plane[2 + j][:].indirect(entries(s * PIECE, PIECE)))
 
-        for s in range(PIECES):
-            pairs = high[s][:].rearrange("p j n -> p n j")
-            if s == PIECES - 1:
-                nc.vector.tensor_copy(woven[s][:, :, 2:4], pairs)
-            else:
-                nc.scalar.copy(woven[s][:, :, 2:4], pairs)
+        for s in range(PIECES - 1):
+            nc.scalar.copy(woven[s][:, :, 2:4], high[s][:].rearrange("p j n -> p n j"))
 
         y = sb.tile([P, S], F32, name="y")
         order = [0, 1, 3, 2]
@@ -95,33 +92,32 @@ def tile_picked_huber_none_e_kernel(tc, xT, w1, bound, offs, cen, pos1, pos2, ou
                 stop=True,
             )
             if s == order[-1]:
-                nc.vector.tensor_copy(y[:, s * PIECE : (s + 1) * PIECE], acc[:])
+                nc.vector.tensor_scalar(y[:, s * PIECE : (s + 1) * PIECE], acc[:], 0.5, None, ALU.mult)
             else:
-                nc.scalar.copy(y[:, s * PIECE : (s + 1) * PIECE], acc[:])
-
-        b_half = sb.tile([P, V], F32, name="b_half")
-        nc.vector.tensor_scalar(b_half[:], b_t[:], 0.5, None, ALU.mult)
+                nc.scalar.activation(y[:, s * PIECE : (s + 1) * PIECE], acc[:], mybir.ActivationFunctionType.Copy, scale=0.5)
 
         centre = sb.tile([P, V], F32, name="centre")
-        near = [sb.tile([P, V], F32, name=f"near{d}") for d in range(2)]
+        near = sb.tile([P, 2, V], F32, name="near")
         upper = sb.tile([P, V], F32, name="upper")
-        lower_half = sb.tile([P, V], F32, name="lower_half")
+        lower = sb.tile([P, V], F32, name="lower")
         nc.vector.tensor_copy(centre[:], y[:].indirect(cen_t[:]))
-        nc.vector.tensor_copy(near[0][:], y[:].indirect(pos1_t[:]))
-        nc.vector.tensor_tensor(upper[:], centre[:], b_t[:], ALU.add)
-        nc.vector.tensor_copy(near[1][:], y[:].indirect(pos2_t[:]))
-        nc.vector.scalar_tensor_tensor(lower_half[:], centre[:], 0.5, b_half[:], ALU.mult, ALU.subtract)
-        capped = [sb.tile([P, V], F32, name=f"capped{d}") for d in range(2)]
-        for d in range(2):
-            nc.vector.tensor_tensor(capped[d][:], near[d][:], upper[:], ALU.min)
-        first_half = sb.tile([P, V], F32, name="first_half")
-        nc.vector.scalar_tensor_tensor(first_half[:], capped[0][:], 0.5, lower_half[:], ALU.mult, ALU.max)
+        nc.vector.tensor_copy(near[:, 0, :], y[:].indirect(pos1_t[:]))
+        nc.vector.scalar_tensor_tensor(upper[:], b_t[:], 0.5, centre[:], ALU.mult, ALU.add)
+        nc.vector.tensor_copy(near[:, 1, :], y[:].indirect(pos2_t[:]))
+        nc.vector.scalar_tensor_tensor(lower[:], b_t[:], -0.5, centre[:], ALU.mult, ALU.add)
         cols = [slice(0, V // 2), slice(V // 2, V)]
-        second_half = [sb.tile([P, V // 2], F32, name=f"second_half{h}") for h in range(2)]
+
+        def for_both(limit, h):
+            return limit[:, cols[h]].unsqueeze(1).to_broadcast([P, 2, V // 2])
+
+        capped = [sb.tile([P, 2, V // 2], F32, name=f"capped{h}") for h in range(2)]
+        clamped = [sb.tile([P, 2, V // 2], F32, name=f"clamped{h}") for h in range(2)]
         for h in range(2):
-            nc.vector.scalar_tensor_tensor(second_half[h][:], capped[1][:, cols[h]], 0.5, lower_half[:, cols[h]], ALU.mult, ALU.max)
+            nc.vector.tensor_tensor(capped[h][:], near[:, :, cols[h]], for_both(upper, h), ALU.min)
+        for h in range(2):
+            nc.vector.tensor_tensor(clamped[h][:], capped[h][:], for_both(lower, h), ALU.max)
         queues = [nc.scalar, nc.sync]
         for h in range(2):
             result = sb.tile([P, V // 2], F32, name=f"result{h}")
-            nc.vector.tensor_tensor(result[:], first_half[:, cols[h]], second_half[h][:], ALU.add)
+            nc.vector.tensor_tensor(result[:], clamped[h][:, 0, :], clamped[h][:, 1, :], ALU.add)
             queues[h].dma_start(out[:, cols[h]], result[:])

@@ -26,6 +26,7 @@ def tile_picked_huber_none_e_kernel(tc, xT, w1, bound, offs, cen, pos1, pos2, ou
     with ExitStack() as ctx:
         lists = ctx.enter_context(tc.tile_pool(name="lists", bufs=1))
         sb = ctx.enter_context(tc.tile_pool(name="sb", bufs=1))
+        reuse = ctx.enter_context(tc.tile_pool(name="reuse", bufs=1))
         ps = ctx.enter_context(tc.psum_pool(name="ps", bufs=1))
 
         offs_t = lists.tile([P, S // PER_COL], U16, name="offs_t")
@@ -35,13 +36,15 @@ def tile_picked_huber_none_e_kernel(tc, xT, w1, bound, offs, cen, pos1, pos2, ou
 
         x_rows = xT.rearrange("(p j) t -> p j t", j=PACK)
         plane = [sb.tile([P, T], F32, name=f"plane{j}") for j in range(PACK)]
-        w_raw = sb.tile([P, PACK, N], F32, name="w_raw")
+        w_room = reuse.tile([P, 3 * PIECE * PACK // 2], F32, name="w_room", align_bytes=64, offset=0)
+        w_raw = w_room[:, 0 : PACK * N]
         b_t = sb.tile([P, V], F32, name="b_t")
 
         nc.sync.dma_start(plane[0][:], x_rows[:, 0, :])
         nc.sync.dma_start(offs_t[:], offs)
-        nc.sync.dma_start(w_raw[:], w1.rearrange("(p j) m -> p j m", j=PACK))
-        for j in range(1, PACK):
+        nc.sync.dma_start(plane[1][:], x_rows[:, 1, :])
+        nc.sync.dma_start(w_raw, w1.rearrange("(p j) m -> p (j m)", j=PACK))
+        for j in range(2, PACK):
             nc.sync.dma_start(plane[j][:], x_rows[:, j, :])
         nc.sync.dma_start(cen_t[:], cen)
         nc.sync.dma_start(pos1_t[:], pos1)
@@ -51,29 +54,30 @@ def tile_picked_huber_none_e_kernel(tc, xT, w1, bound, offs, cen, pos1, pos2, ou
         def entries(first, count):
             return offs_t[:, first // PER_COL : (first + count) // PER_COL]
 
-        low = [sb.tile([P, 2, HALF], F32, name=f"low{h}") for h in range(2)]
-        high = [sb.tile([P, 2, PIECE], F32, name=f"high{s}") for s in range(PIECES - 1)]
-        woven = [sb.tile([P, PIECE, PACK], BF16, name=f"woven{s}", align_bytes=64) for s in range(PIECES)]
+        staged = S - PIECE
+        low = sb.tile([P, 2, S], F32, name="low")
+        high = reuse.tile([P, 2, staged], F32, name="high", align_bytes=64, offset=4 * PIECE * PACK * 2)
+        woven = [reuse.tile([P, PIECE, PACK], BF16, name=f"woven{s}", align_bytes=64, offset=s * PIECE * PACK * 2) for s in range(PIECES)]
 
-        w_woven = sb.tile([P, N, PACK], BF16, name="w_woven", align_bytes=64)
+        w_woven_room = reuse.tile([P, 2 * N * PACK], BF16, name="w_woven_room", align_bytes=64, offset=3 * PIECE * PACK * 2)
+        w_woven = w_woven_room[:, 0 : N * PACK]
         w_codes = sb.tile([P, N], U32, name="w_codes", align_bytes=64)
         w_scales = sb.tile([P, N], U8, name="w_scales", align_bytes=64)
-        nc.scalar.copy(w_woven[:], w_raw[:].rearrange("p j m -> p m j"))
-        nc.vector.quantize_mx(out=w_codes[:].bitcast(FP8X4), scales=w_scales[:], in_=w_woven[:].rearrange("p m j -> p (m j)"))
+        nc.scalar.copy(w_woven.rearrange("p (m j) -> p m j", j=PACK), w_raw.rearrange("p (j m) -> p m j", j=PACK))
+        nc.vector.quantize_mx(out=w_codes[:].bitcast(FP8X4), scales=w_scales[:], in_=w_woven)
 
-        for j in range(2):
-            for h in range(2):
-                nc.vector.tensor_copy(low[h][:, j, :], plane[j][:].indirect(entries(h * HALF, HALF)))
+        nc.vector.tensor_copy(low[:, 0, :], plane[0][:].indirect(offs_t[:]))
+        for h in range(2):
+            nc.vector.tensor_copy(low[:, 1, h * HALF : (h + 1) * HALF], plane[1][:].indirect(entries(h * HALF, HALF)))
         for s in range(PIECES):
-            h, first = divmod(s * PIECE, HALF)
-            nc.scalar.copy(woven[s][:, :, 0:2], low[h][:, :, first : first + PIECE].rearrange("p j n -> p n j"))
-        for j in range(2):
-            for s in range(PIECES):
-                target = woven[s][:, :, 2 + j] if s == PIECES - 1 else high[s][:, j, :]
-                nc.vector.tensor_copy(target, plane[2 + j][:].indirect(entries(s * PIECE, PIECE)))
-
+            nc.scalar.copy(woven[s][:, :, 0:2], low[:, :, s * PIECE : (s + 1) * PIECE].rearrange("p j n -> p n j"))
+        nc.vector.tensor_copy(high[:, 0, :], plane[2][:].indirect(entries(0, staged)))
+        nc.vector.tensor_copy(woven[PIECES - 1][:, :, 2], plane[2][:].indirect(entries(staged, PIECE)))
         for s in range(PIECES - 1):
-            nc.scalar.copy(woven[s][:, :, 2:4], high[s][:].rearrange("p j n -> p n j"))
+            nc.vector.tensor_copy(high[:, 1, s * PIECE : (s + 1) * PIECE], plane[3][:].indirect(entries(s * PIECE, PIECE)))
+        nc.vector.tensor_copy(woven[PIECES - 1][:, :, 3], plane[3][:].indirect(entries(staged, PIECE)))
+        for s in range(PIECES - 1):
+            nc.scalar.copy(woven[s][:, :, 2:4], high[:, :, s * PIECE : (s + 1) * PIECE].rearrange("p j n -> p n j"))
 
         y = sb.tile([P, S], F32, name="y")
         order = [0, 1, 3, 2]

@@ -96,32 +96,36 @@ def tile_picked_huber_none_e_kernel(tc, xT, w1, bound, offs, cen, pos1, pos2, ou
                 stop=True,
             )
             if s == order[-1]:
-                nc.vector.tensor_scalar(y[:, s * PIECE : (s + 1) * PIECE], acc[:], 0.5, None, ALU.mult)
+                nc.vector.tensor_copy(y[:, s * PIECE : (s + 1) * PIECE], acc[:])
             else:
-                nc.scalar.activation(y[:, s * PIECE : (s + 1) * PIECE], acc[:], mybir.ActivationFunctionType.Copy, scale=0.5)
+                nc.scalar.copy(y[:, s * PIECE : (s + 1) * PIECE], acc[:])
 
-        centre = sb.tile([P, V], F32, name="centre")
-        near = sb.tile([P, 2, V], F32, name="near")
-        upper = sb.tile([P, V], F32, name="upper")
-        lower = sb.tile([P, V], F32, name="lower")
-        nc.vector.tensor_copy(centre[:], y[:].indirect(cen_t[:]))
-        nc.vector.tensor_copy(near[:, 0, :], y[:].indirect(pos1_t[:]))
-        nc.vector.scalar_tensor_tensor(upper[:], b_t[:], 0.5, centre[:], ALU.mult, ALU.add)
-        nc.vector.tensor_copy(near[:, 1, :], y[:].indirect(pos2_t[:]))
-        nc.vector.scalar_tensor_tensor(lower[:], b_t[:], -0.5, centre[:], ALU.mult, ALU.add)
-        cols = [slice(0, V // 2), slice(V // 2, V)]
+        floor = reuse.tile([P, V], F32, name="floor", align_bytes=64, offset=order[-1] * PIECE * PACK * 2)
+        nc.vector.tensor_scalar(floor[:], b_t[:], -2.0, None, ALU.mult)
 
-        def for_both(limit, h):
-            return limit[:, cols[h]].unsqueeze(1).to_broadcast([P, 2, V // 2])
+        part = V // 2
+        cols = [slice(0, part), slice(part, V)]
 
-        capped = [sb.tile([P, 2, V // 2], F32, name=f"capped{h}") for h in range(2)]
-        clamped = [sb.tile([P, 2, V // 2], F32, name=f"clamped{h}") for h in range(2)]
+        def targets(lst, h):
+            return lst[:, h * part // PER_COL : (h + 1) * part // PER_COL]
+
+        upper = [sb.tile([P, part], F32, name=f"upper{h}") for h in range(2)]
+        excess = [sb.tile([P, 2, part], F32, name=f"excess{h}") for h in range(2)]
+        pull = [sb.tile([P, 2, part], F32, name=f"pull{h}") for h in range(2)]
+        both = [sb.tile([P, part], F32, name=f"both{h}") for h in range(2)]
         for h in range(2):
-            nc.vector.tensor_tensor(capped[h][:], near[:, :, cols[h]], for_both(upper, h), ALU.min)
+            nc.vector.tensor_tensor(upper[h][:], y[:].indirect(targets(cen_t, h)), b_t[:, cols[h]], ALU.add)
         for h in range(2):
-            nc.vector.tensor_tensor(clamped[h][:], capped[h][:], for_both(lower, h), ALU.max)
+            for i, lst in enumerate((pos1_t, pos2_t)):
+                nc.vector.tensor_tensor(excess[h][:, i, :], y[:].indirect(targets(lst, h)), upper[h][:], ALU.subtract)
+        for h in range(2):
+            nc.vector.scalar_tensor_tensor(
+                pull[h][:], excess[h][:], 0.0, floor[:, cols[h]].unsqueeze(1).to_broadcast([P, 2, part]), ALU.min, ALU.max
+            )
+        for h in range(2):
+            nc.vector.tensor_tensor(both[h][:], pull[h][:, 0, :], pull[h][:, 1, :], ALU.add)
         queues = [nc.scalar, nc.sync]
         for h in range(2):
-            result = sb.tile([P, V // 2], F32, name=f"result{h}")
-            nc.vector.tensor_tensor(result[:], clamped[h][:, 0, :], clamped[h][:, 1, :], ALU.add)
+            result = sb.tile([P, part], F32, name=f"result{h}")
+            nc.vector.scalar_tensor_tensor(result[:], both[h][:], 0.5, upper[h][:], ALU.mult, ALU.add)
             queues[h].dma_start(out[:, cols[h]], result[:])

@@ -36,56 +36,65 @@ def tile_picked_huber_none_e_kernel(tc, xT, w1, bound, offs, cen, pos1, pos2, ou
 
         x_rows = xT.rearrange("(p j) t -> p j t", j=PACK)
         plane = [sb.tile([P, T], F32, name=f"plane{j}") for j in range(PACK)]
-        w_room = reuse.tile([P, 3 * PIECE * PACK // 2], F32, name="w_room", align_bytes=64, offset=0)
-        w_raw = w_room[:, 0 : PACK * N]
+        w_at, last_at = 0, 2048
+        w_raw = reuse.tile([P, PACK * N], F32, name="w_raw", align_bytes=64, offset=w_at)
         b_t = sb.tile([P, V], F32, name="b_t")
 
-        nc.sync.dma_start(plane[0][:], x_rows[:, 0, :])
+        nc.sync.dma_start(plane[2][:], x_rows[:, 2, :])
         nc.sync.dma_start(offs_t[:], offs)
-        nc.sync.dma_start(plane[1][:], x_rows[:, 1, :])
-        nc.sync.dma_start(w_raw, w1.rearrange("(p j) m -> p (j m)", j=PACK))
-        for j in range(2, PACK):
+        for j in (0, 1, 3):
             nc.sync.dma_start(plane[j][:], x_rows[:, j, :])
+        nc.sync.dma_start(w_raw[:], w1.rearrange("(p j) m -> p (j m)", j=PACK))
         nc.sync.dma_start(cen_t[:], cen)
+        nc.sync.dma_start(b_t[:], bound)
         nc.sync.dma_start(pos1_t[:], pos1)
         nc.sync.dma_start(pos2_t[:], pos2)
-        nc.sync.dma_start(b_t[:], bound)
 
-        def entries(first, count):
-            return offs_t[:, first // PER_COL : (first + count) // PER_COL]
+        def picked(j, s, count=1):
+            return plane[j][:].indirect(offs_t[:, s * PIECE // PER_COL : (s + count) * PIECE // PER_COL])
 
-        staged = S - PIECE
-        low = sb.tile([P, 2, S], F32, name="low")
-        high = reuse.tile([P, 2, staged], F32, name="high", align_bytes=64, offset=4 * PIECE * PACK * 2)
-        woven = [reuse.tile([P, PIECE, PACK], BF16, name=f"woven{s}", align_bytes=64, offset=s * PIECE * PACK * 2) for s in range(PIECES)]
+        front = sb.tile([P, PACK, HALF], F32, name="front")
+        back = sb.tile([P, 2, HALF], F32, name="back")
+        woven0 = sb.tile([P, PIECE, PACK], BF16, name="woven0", align_bytes=64)
+        woven1 = reuse.tile([P, PIECE, PACK], BF16, name="woven1", align_bytes=64, offset=last_at)
+        woven23 = sb.tile([P, HALF, PACK], BF16, name="woven23", align_bytes=64)
+        woven = [woven0, woven1]
 
-        w_woven_room = reuse.tile([P, 2 * N * PACK], BF16, name="w_woven_room", align_bytes=64, offset=3 * PIECE * PACK * 2)
-        w_woven = w_woven_room[:, 0 : N * PACK]
+        def piece(s):
+            return slice(s * PIECE, (s + 1) * PIECE)
+
+        def weave_front(s, first):
+            nc.scalar.copy(woven[s][:, :, first:PACK:2], front[:, first:PACK:2, piece(s)].rearrange("p j n -> p n j"))
+
+        nc.vector.tensor_copy(front[:, 2, :], picked(2, 0, 2))
+        nc.vector.tensor_copy(woven23[:, :, 2], picked(2, 2, 2))
+        nc.vector.tensor_copy(front[:, 0, :], picked(0, 0, 2))
+        nc.vector.tensor_copy(back[:, 0, :], picked(0, 2, 2))
+        for s in range(2):
+            weave_front(s, 0)
+        for s in range(2):
+            nc.vector.tensor_copy(back[:, 1, piece(s)], picked(1, 2 + s))
+            nc.scalar.copy(woven23[:, piece(s), 0:2], back[:, :, piece(s)].rearrange("p j n -> p n j"))
+        nc.vector.tensor_copy(front[:, 1, :], picked(1, 0, 2))
+        for s in range(2):
+            nc.vector.tensor_copy(front[:, 3, piece(s)], picked(3, s))
+        nc.vector.tensor_copy(woven23[:, :, 3], picked(3, 2, 2))
+
+        w_woven = sb.tile([P, N, PACK], BF16, name="w_woven", align_bytes=64)
         w_codes = sb.tile([P, N], U32, name="w_codes", align_bytes=64)
         w_scales = sb.tile([P, N], U8, name="w_scales", align_bytes=64)
-        nc.scalar.copy(w_woven.rearrange("p (m j) -> p m j", j=PACK), w_raw.rearrange("p (j m) -> p m j", j=PACK))
-        nc.vector.quantize_mx(out=w_codes[:].bitcast(FP8X4), scales=w_scales[:], in_=w_woven)
-
-        nc.vector.tensor_copy(low[:, 0, :], plane[0][:].indirect(offs_t[:]))
-        for h in range(2):
-            nc.vector.tensor_copy(low[:, 1, h * HALF : (h + 1) * HALF], plane[1][:].indirect(entries(h * HALF, HALF)))
-        for s in range(PIECES):
-            nc.scalar.copy(woven[s][:, :, 0:2], low[:, :, s * PIECE : (s + 1) * PIECE].rearrange("p j n -> p n j"))
-        nc.vector.tensor_copy(high[:, 0, :], plane[2][:].indirect(entries(0, staged)))
-        nc.vector.tensor_copy(woven[PIECES - 1][:, :, 2], plane[2][:].indirect(entries(staged, PIECE)))
-        for s in range(PIECES - 1):
-            nc.vector.tensor_copy(high[:, 1, s * PIECE : (s + 1) * PIECE], plane[3][:].indirect(entries(s * PIECE, PIECE)))
-        nc.vector.tensor_copy(woven[PIECES - 1][:, :, 3], plane[3][:].indirect(entries(staged, PIECE)))
-        for s in range(PIECES - 1):
-            nc.scalar.copy(woven[s][:, :, 2:4], high[:, :, s * PIECE : (s + 1) * PIECE].rearrange("p j n -> p n j"))
+        weave_front(0, 1)
+        nc.scalar.copy(w_woven[:], w_raw[:].rearrange("p (j m) -> p m j", j=PACK))
+        weave_front(1, 1)
+        nc.vector.quantize_mx(out=w_codes[:].bitcast(FP8X4), scales=w_scales[:], in_=w_woven[:].rearrange("p m j -> p (m j)"))
 
         y = sb.tile([P, S], F32, name="y")
-        order = [0, 1, 3, 2]
-        for s in order:
-            codes = sb.tile([P, PIECE], U32, name=f"codes{s}", align_bytes=64)
-            scales = sb.tile([P, PIECE], U8, name=f"scales{s}", align_bytes=64)
-            nc.vector.quantize_mx(out=codes[:].bitcast(FP8X4), scales=scales[:], in_=woven[s][:].rearrange("p n j -> p (n j)"))
-            acc = ps.tile([P, PIECE], F32, name=f"acc{s}")
+        groups = [(woven23, HALF, HALF), (woven0, 0, PIECE), (woven1, PIECE, PIECE)]
+        for g, (source, first, width) in enumerate(groups):
+            codes = reuse.tile([P, width], U32, name=f"codes{g}", align_bytes=64, offset=w_at + 4 * ((first + HALF) % S))
+            scales = sb.tile([P, width], U8, name=f"scales{g}", align_bytes=64)
+            nc.vector.quantize_mx(out=codes[:].bitcast(FP8X4), scales=scales[:], in_=source[:].rearrange("p n j -> p (n j)"))
+            acc = ps.tile([P, width], F32, name=f"acc{g}")
             nc.tensor.matmul_mx(
                 out=acc[:],
                 lhsT=w_codes[:].bitcast(FP8X4),
@@ -95,12 +104,12 @@ def tile_picked_huber_none_e_kernel(tc, xT, w1, bound, offs, cen, pos1, pos2, ou
                 start=True,
                 stop=True,
             )
-            if s == order[-1]:
-                nc.vector.tensor_copy(y[:, s * PIECE : (s + 1) * PIECE], acc[:])
+            if g == len(groups) - 1:
+                nc.vector.tensor_copy(y[:, first : first + width], acc[:])
             else:
-                nc.scalar.copy(y[:, s * PIECE : (s + 1) * PIECE], acc[:])
+                nc.scalar.copy(y[:, first : first + width], acc[:])
 
-        floor = reuse.tile([P, V], F32, name="floor", align_bytes=64, offset=order[-1] * PIECE * PACK * 2)
+        floor = reuse.tile([P, V], F32, name="floor", align_bytes=64, offset=last_at)
         nc.vector.tensor_scalar(floor[:], b_t[:], -2.0, None, ALU.mult)
 
         part = V // 2

@@ -76,22 +76,27 @@ def tile_picked_huber_none_e_kernel(tc, xT, w1, bound, offs, cen, pos1, pos2, ou
             nc.vector.tensor_copy(back[:, 1, piece(s)], picked(1, 2 + s))
             nc.scalar.copy(woven23[:, piece(s), 0:2], back[:, :, piece(s)].rearrange("p j n -> p n j"))
         nc.vector.tensor_copy(front[:, 1, :], picked(1, 0, 2))
-        for s in range(2):
-            nc.vector.tensor_copy(front[:, 3, piece(s)], picked(3, s))
+        nc.vector.tensor_copy(front[:, 3, piece(0)], picked(3, 0))
         nc.vector.tensor_copy(woven23[:, :, 3], picked(3, 2, 2))
+        nc.vector.tensor_copy(front[:, 3, piece(1)], picked(3, 1))
 
         w_woven = sb.tile([P, N, PACK], BF16, name="w_woven", align_bytes=64)
         w_codes = sb.tile([P, N], U32, name="w_codes", align_bytes=64)
         w_scales = sb.tile([P, N], U8, name="w_scales", align_bytes=64)
         weave_front(0, 1)
-        nc.scalar.copy(w_woven[:], w_raw[:].rearrange("p (j m) -> p m j", j=PACK))
+        nc.scalar.copy(
+            w_woven[:].rearrange("p (c i) j -> p c j i", i=4), w_raw[:].rearrange("p (j c i) -> p c j i", j=PACK, i=4)
+        )
         weave_front(1, 1)
         nc.vector.quantize_mx(out=w_codes[:].bitcast(FP8X4), scales=w_scales[:], in_=w_woven[:].rearrange("p m j -> p (m j)"))
 
         y = sb.tile([P, S], F32, name="y")
         groups = [(woven23, HALF, HALF), (woven0, 0, PIECE), (woven1, PIECE, PIECE)]
         for g, (source, first, width) in enumerate(groups):
-            codes = reuse.tile([P, width], U32, name=f"codes{g}", align_bytes=64, offset=w_at + 4 * ((first + HALF) % S))
+            if g == 0:
+                codes = sb.tile([P, width], U32, name=f"codes{g}", align_bytes=64)
+            else:
+                codes = reuse.tile([P, width], U32, name=f"codes{g}", align_bytes=64, offset=w_at + 4 * first)
             scales = sb.tile([P, width], U8, name=f"scales{g}", align_bytes=64)
             nc.vector.quantize_mx(out=codes[:].bitcast(FP8X4), scales=scales[:], in_=source[:].rearrange("p n j -> p (n j)"))
             acc = ps.tile([P, width], F32, name=f"acc{g}")

@@ -123,23 +123,34 @@ def tile_picked_huber_none_e_kernel(tc, xT, w1, bound, offs, cen, pos1, pos2, ou
         def targets(lst, h):
             return lst[:, h * part // PER_COL : (h + 1) * part // PER_COL]
 
-        upper = [sb.tile([P, part], F32, name=f"upper{h}") for h in range(2)]
-        excess = [sb.tile([P, 2, part], F32, name=f"excess{h}") for h in range(2)]
-        pull = [sb.tile([P, 2, part], F32, name=f"pull{h}") for h in range(2)]
-        both = [sb.tile([P, part], F32, name=f"both{h}") for h in range(2)]
+        def halves(name):
+            return [sb.tile([P, part], F32, name=f"{name}{h}") for h in range(2)]
+
+        upper, excess1, excess2 = halves("upper"), halves("excess1"), halves("excess2")
+        pull1, pull2, partial, result = halves("pull1"), halves("pull2"), halves("partial"), halves("result")
+
+        def fetch(dst, lst, other, op, h):
+            nc.vector.tensor_tensor(dst[h][:], y[:].indirect(targets(lst, h)), other, op)
+
+        def clip(dst, src, h):
+            nc.vector.scalar_tensor_tensor(dst[h][:], src[h][:], 0.0, floor[:, cols[h]], ALU.min, ALU.max)
+
+        def add_half(dst, pull, base, h):
+            nc.vector.scalar_tensor_tensor(dst[h][:], pull[h][:], 0.5, base[h][:], ALU.mult, ALU.add)
+
         for h in range(2):
-            nc.vector.tensor_tensor(upper[h][:], y[:].indirect(targets(cen_t, h)), b_t[:, cols[h]], ALU.add)
+            fetch(upper, cen_t, b_t[:, cols[h]], ALU.add, h)
         for h in range(2):
-            for i, lst in enumerate((pos1_t, pos2_t)):
-                nc.vector.tensor_tensor(excess[h][:, i, :], y[:].indirect(targets(lst, h)), upper[h][:], ALU.subtract)
-        for h in range(2):
-            nc.vector.scalar_tensor_tensor(
-                pull[h][:], excess[h][:], 0.0, floor[:, cols[h]].unsqueeze(1).to_broadcast([P, 2, part]), ALU.min, ALU.max
-            )
-        for h in range(2):
-            nc.vector.tensor_tensor(both[h][:], pull[h][:, 0, :], pull[h][:, 1, :], ALU.add)
+            fetch(excess1, pos1_t, upper[h][:], ALU.subtract, h)
+        clip(pull1, excess1, 0)
+        fetch(excess2, pos2_t, upper[0][:], ALU.subtract, 0)
+        clip(pull1, excess1, 1)
+        add_half(partial, pull1, upper, 0)
+        fetch(excess2, pos2_t, upper[1][:], ALU.subtract, 1)
+        clip(pull2, excess2, 0)
+        add_half(partial, pull1, upper, 1)
+        clip(pull2, excess2, 1)
         queues = [nc.scalar, nc.sync]
         for h in range(2):
-            result = sb.tile([P, part], F32, name=f"result{h}")
-            nc.vector.scalar_tensor_tensor(result[:], both[h][:], 0.5, upper[h][:], ALU.mult, ALU.add)
-            queues[h].dma_start(out[:, cols[h]], result[:])
+            add_half(result, pull2, partial, h)
+            queues[h].dma_start(out[:, cols[h]], result[h][:])

@@ -91,14 +91,19 @@ def tile_picked_huber_none_e_kernel(tc, xT, w1, bound, offs, cen, pos1, pos2, ou
         nc.vector.quantize_mx(out=w_codes[:].bitcast(FP8X4), scales=w_scales[:], in_=w_woven[:].rearrange("p m j -> p (m j)"))
 
         y = sb.tile([P, S], F32, name="y")
-        groups = [(woven23, HALF, HALF), (woven0, 0, PIECE), (woven1, PIECE, PIECE)]
+        groups = [
+            (woven23[:, piece(0), :], 2 * PIECE, PIECE),
+            (woven23[:, piece(1), :], 3 * PIECE, PIECE),
+            (woven0[:], 0, PIECE),
+            (woven1[:], PIECE, PIECE),
+        ]
         for g, (source, first, width) in enumerate(groups):
             if g == 0:
                 codes = sb.tile([P, width], U32, name=f"codes{g}", align_bytes=64)
             else:
                 codes = reuse.tile([P, width], U32, name=f"codes{g}", align_bytes=64, offset=w_at + 4 * first)
             scales = sb.tile([P, width], U8, name=f"scales{g}", align_bytes=64)
-            nc.vector.quantize_mx(out=codes[:].bitcast(FP8X4), scales=scales[:], in_=source[:].rearrange("p n j -> p (n j)"))
+            nc.vector.quantize_mx(out=codes[:].bitcast(FP8X4), scales=scales[:], in_=source.rearrange("p n j -> p (n j)"))
             acc = ps.tile([P, width], F32, name=f"acc{g}")
             nc.tensor.matmul_mx(
                 out=acc[:],

@@ -40,9 +40,9 @@ def tile_picked_huber_none_e_kernel(tc, xT, w1, bound, offs, cen, pos1, pos2, ou
         w_raw = reuse.tile([P, PACK * N], F32, name="w_raw", align_bytes=64, offset=w_at)
         b_t = sb.tile([P, V], F32, name="b_t")
 
-        nc.sync.dma_start(plane[2][:], x_rows[:, 2, :])
+        nc.sync.dma_start(plane[0][:], x_rows[:, 0, :])
         nc.sync.dma_start(offs_t[:], offs)
-        for j in (0, 1, 3):
+        for j in (2, 3, 1):
             nc.sync.dma_start(plane[j][:], x_rows[:, j, :])
         nc.sync.dma_start(w_raw[:], w1.rearrange("(p j) m -> p (j m)", j=PACK))
         nc.sync.dma_start(cen_t[:], cen)
@@ -53,49 +53,47 @@ def tile_picked_huber_none_e_kernel(tc, xT, w1, bound, offs, cen, pos1, pos2, ou
         def picked(j, s, count=1):
             return plane[j][:].indirect(offs_t[:, s * PIECE // PER_COL : (s + count) * PIECE // PER_COL])
 
-        front = sb.tile([P, PACK, HALF], F32, name="front")
-        back = sb.tile([P, 2, HALF], F32, name="back")
-        woven0 = sb.tile([P, PIECE, PACK], BF16, name="woven0", align_bytes=64)
-        woven1 = reuse.tile([P, PIECE, PACK], BF16, name="woven1", align_bytes=64, offset=last_at)
+        stage = sb.tile([P, PACK - 1, S], F32, name="stage")
+        woven01 = reuse.tile([P, HALF, PACK], BF16, name="woven01", align_bytes=64, offset=last_at)
         woven23 = sb.tile([P, HALF, PACK], BF16, name="woven23", align_bytes=64)
-        woven = [woven0, woven1]
+        rounded = sb.tile([P, T], BF16, name="rounded")
 
         def piece(s):
             return slice(s * PIECE, (s + 1) * PIECE)
 
-        def weave_front(s, first):
-            nc.scalar.copy(woven[s][:, :, first:PACK:2], front[:, first:PACK:2, piece(s)].rearrange("p j n -> p n j"))
+        def weave_front(s):
+            nc.scalar.copy(woven01[:, piece(s), 1:PACK], stage[:, :, piece(s)].rearrange("p j n -> p n j"))
 
-        nc.vector.tensor_copy(front[:, 2, :], picked(2, 0, 2))
-        nc.vector.tensor_copy(woven23[:, :, 2], picked(2, 2, 2))
-        nc.vector.tensor_copy(front[:, 0, :], picked(0, 0, 2))
-        nc.vector.tensor_copy(back[:, 0, :], picked(0, 2, 2))
+        nc.scalar.copy(rounded[:], plane[0][:])
+        nc.scalar.activation(
+            woven01[:, :, 0], rounded[:].indirect(offs_t[:, 0 : HALF // PER_COL]), mybir.ActivationFunctionType.Copy
+        )
+        nc.vector.tensor_copy(woven23[:, :, 0], picked(0, 2, 2))
+        nc.vector.tensor_copy(stage[:, 1, :], picked(2, 0, PIECES))
         for s in range(2):
-            weave_front(s, 0)
-        for s in range(2):
-            nc.vector.tensor_copy(back[:, 1, piece(s)], picked(1, 2 + s))
-            nc.scalar.copy(woven23[:, piece(s), 0:2], back[:, :, piece(s)].rearrange("p j n -> p n j"))
-        nc.vector.tensor_copy(front[:, 1, :], picked(1, 0, 2))
-        nc.vector.tensor_copy(front[:, 3, piece(0)], picked(3, 0))
-        nc.vector.tensor_copy(woven23[:, :, 3], picked(3, 2, 2))
-        nc.vector.tensor_copy(front[:, 3, piece(1)], picked(3, 1))
+            nc.vector.tensor_copy(stage[:, 2, piece(2 + s)], picked(3, 2 + s))
+            nc.scalar.copy(woven23[:, piece(s), 2:PACK], stage[:, 1:3, piece(2 + s)].rearrange("p j n -> p n j"))
+        nc.vector.tensor_copy(stage[:, 2, 0:HALF], picked(3, 0, 2))
+        nc.vector.tensor_copy(stage[:, 0, piece(0)], picked(1, 0))
+        nc.vector.tensor_copy(woven23[:, :, 1], picked(1, 2, 2))
+        nc.vector.tensor_copy(stage[:, 0, piece(1)], picked(1, 1))
 
         w_woven = sb.tile([P, N, PACK], BF16, name="w_woven", align_bytes=64)
         w_codes = sb.tile([P, N], U32, name="w_codes", align_bytes=64)
         w_scales = sb.tile([P, N], U8, name="w_scales", align_bytes=64)
-        weave_front(0, 1)
+        weave_front(0)
         nc.scalar.copy(
             w_woven[:].rearrange("p (c i) j -> p c j i", i=4), w_raw[:].rearrange("p (j c i) -> p c j i", j=PACK, i=4)
         )
-        weave_front(1, 1)
+        weave_front(1)
         nc.vector.quantize_mx(out=w_codes[:].bitcast(FP8X4), scales=w_scales[:], in_=w_woven[:].rearrange("p m j -> p (m j)"))
 
         y = sb.tile([P, S], F32, name="y")
         groups = [
             (woven23[:, piece(0), :], 2 * PIECE, PIECE),
             (woven23[:, piece(1), :], 3 * PIECE, PIECE),
-            (woven0[:], 0, PIECE),
-            (woven1[:], PIECE, PIECE),
+            (woven01[:, piece(0), :], 0, PIECE),
+            (woven01[:, piece(1), :], PIECE, PIECE),
         ]
         for g, (source, first, width) in enumerate(groups):
             if g == 0:

@@ -153,7 +153,7 @@ def tile_picked_huber_none_e_kernel(tc, xT, w1, bound, offs, cen, pos1, pos2, ou
         clip(pull2, excess2, 0)
         add_half(partial, pull1, upper, 1)
         clip(pull2, excess2, 1)
-        queues = [nc.scalar, nc.sync]
+        queues = [nc.sync, nc.sync]
         for h in range(2):
             add_half(result, pull2, partial, h)
             queues[h].dma_start(out[:, cols[h]], result[h][:])

@@ -38,62 +38,60 @@ def tile_picked_huber_none_e_kernel(tc, xT, w1, bound, offs, cen, pos1, pos2, ou
         plane = [sb.tile([P, T], F32, name=f"plane{j}") for j in range(PACK)]
         w_at, last_at = 0, 2048
         w_raw = reuse.tile([P, PACK * N], F32, name="w_raw", align_bytes=64, offset=w_at)
-        b_t = sb.tile([P, V], F32, name="b_t")
+        stage = sb.tile([P, PACK - 1, S + 2 * V], BF16, name="stage")
+        b_t = stage[:, 0, S : S + 2 * V].bitcast(F32)
 
         nc.sync.dma_start(plane[0][:], x_rows[:, 0, :])
         nc.sync.dma_start(offs_t[:], offs)
         for j in (2, 3, 1):
             nc.sync.dma_start(plane[j][:], x_rows[:, j, :])
         nc.sync.dma_start(w_raw[:], w1.rearrange("(p j) m -> p (j m)", j=PACK))
+        nc.sync.dma_start(b_t, bound)
         nc.sync.dma_start(cen_t[:], cen)
-        nc.sync.dma_start(b_t[:], bound)
         nc.sync.dma_start(pos1_t[:], pos1)
         nc.sync.dma_start(pos2_t[:], pos2)
 
         def picked(j, s, count=1):
             return plane[j][:].indirect(offs_t[:, s * PIECE // PER_COL : (s + count) * PIECE // PER_COL])
 
-        stage = sb.tile([P, PACK - 1, S], F32, name="stage")
-        woven01 = reuse.tile([P, HALF, PACK], BF16, name="woven01", align_bytes=64, offset=last_at)
-        woven23 = sb.tile([P, HALF, PACK], BF16, name="woven23", align_bytes=64)
+        woven_s = reuse.tile([P, PIECE, PACK], BF16, name="woven_s", align_bytes=64, offset=last_at)
+        woven_v = sb.tile([P, S - PIECE, PACK], BF16, name="woven_v", align_bytes=64)
         rounded = sb.tile([P, T], BF16, name="rounded")
 
-        def piece(s):
-            return slice(s * PIECE, (s + 1) * PIECE)
-
-        def weave_front(s):
-            nc.scalar.copy(woven01[:, piece(s), 1:PACK], stage[:, :, piece(s)].rearrange("p j n -> p n j"))
+        def piece(s, count=1):
+            return slice(s * PIECE, (s + count) * PIECE)
 
         nc.scalar.copy(rounded[:], plane[0][:])
         nc.scalar.activation(
-            woven01[:, :, 0], rounded[:].indirect(offs_t[:, 0 : HALF // PER_COL]), mybir.ActivationFunctionType.Copy
+            woven_s[:, :, 0], rounded[:].indirect(offs_t[:, 0 : PIECE // PER_COL]), mybir.ActivationFunctionType.Copy
         )
-        nc.vector.tensor_copy(woven23[:, :, 0], picked(0, 2, 2))
-        nc.vector.tensor_copy(stage[:, 1, :], picked(2, 0, PIECES))
-        for s in range(2):
-            nc.vector.tensor_copy(stage[:, 2, piece(2 + s)], picked(3, 2 + s))
-            nc.scalar.copy(woven23[:, piece(s), 2:PACK], stage[:, 1:3, piece(2 + s)].rearrange("p j n -> p n j"))
-        nc.vector.tensor_copy(stage[:, 2, 0:HALF], picked(3, 0, 2))
+        nc.vector.tensor_copy(woven_v[:, :, 0], picked(0, 1, 3))
+        nc.vector.tensor_copy(stage[:, 1, 0:S], picked(2, 0, PIECES))
+        for s in range(1, PIECES):
+            nc.vector.tensor_copy(stage[:, 2, piece(s)], picked(3, s))
+            nc.scalar.copy(woven_v[:, piece(s - 1), 2:PACK], stage[:, 1:3, piece(s)].rearrange("p j n -> p n j"))
+        nc.vector.tensor_copy(stage[:, 2, piece(0)], picked(3, 0))
+        nc.vector.tensor_copy(woven_v[:, piece(0, 2), 1], picked(1, 1, 2))
         nc.vector.tensor_copy(stage[:, 0, piece(0)], picked(1, 0))
-        nc.vector.tensor_copy(woven23[:, :, 1], picked(1, 2, 2))
-        nc.vector.tensor_copy(stage[:, 0, piece(1)], picked(1, 1))
+        nc.vector.tensor_copy(woven_v[:, piece(2), 1], picked(1, 3))
 
         w_woven = sb.tile([P, N, PACK], BF16, name="w_woven", align_bytes=64)
         w_codes = sb.tile([P, N], U32, name="w_codes", align_bytes=64)
         w_scales = sb.tile([P, N], U8, name="w_scales", align_bytes=64)
-        weave_front(0)
         nc.scalar.copy(
             w_woven[:].rearrange("p (c i) j -> p c j i", i=4), w_raw[:].rearrange("p (j c i) -> p c j i", j=PACK, i=4)
         )
-        weave_front(1)
+        nc.scalar.copy(woven_s[:, :, 1:PACK], stage[:, :, piece(0)].rearrange("p j n -> p n j"))
         nc.vector.quantize_mx(out=w_codes[:].bitcast(FP8X4), scales=w_scales[:], in_=w_woven[:].rearrange("p m j -> p (m j)"))
 
         y = sb.tile([P, S], F32, name="y")
+        small = PIECE // 2
         groups = [
-            (woven23[:, piece(0), :], 2 * PIECE, PIECE),
-            (woven23[:, piece(1), :], 3 * PIECE, PIECE),
-            (woven01[:, piece(0), :], 0, PIECE),
-            (woven01[:, piece(1), :], PIECE, PIECE),
+            (woven_v[:, piece(0), :], PIECE, PIECE),
+            (woven_v[:, piece(1), :], 2 * PIECE, PIECE),
+            (woven_v[:, piece(2), :], 3 * PIECE, PIECE),
+            (woven_s[:, 0:small, :], 0, small),
+            (woven_s[:, small:PIECE, :], small, small),
         ]
         for g, (source, first, width) in enumerate(groups):
             if g == 0:
@@ -118,7 +116,7 @@ def tile_picked_huber_none_e_kernel(tc, xT, w1, bound, offs, cen, pos1, pos2, ou
                 nc.scalar.copy(y[:, first : first + width], acc[:])
 
         floor = reuse.tile([P, V], F32, name="floor", align_bytes=64, offset=last_at)
-        nc.vector.tensor_scalar(floor[:], b_t[:], -2.0, None, ALU.mult)
+        nc.vector.tensor_scalar(floor[:], b_t, -2.0, None, ALU.mult)
 
         part = V // 2
         cols = [slice(0, part), slice(part, V)]

@@ -78,8 +78,14 @@ def tile_picked_huber_none_e_kernel(tc, xT, w1, bound, offs, cen, pos1, pos2, ou
         w_woven = sb.tile([P, N, PACK], BF16, name="w_woven", align_bytes=64)
         w_codes = sb.tile([P, N], U32, name="w_codes", align_bytes=64)
         w_scales = sb.tile([P, N], U8, name="w_scales", align_bytes=64)
+        cut = 64
+        w_rows = w_raw[:].rearrange("p (j m) -> p j m", j=PACK)
+        nc.gpsimd.tensor_scalar(
+            w_woven[:, 0:cut, :], w_rows[:, :, 0:cut].rearrange("p j m -> p m j"), 1.0, 0.0, ALU.mult, ALU.add
+        )
         nc.scalar.copy(
-            w_woven[:].rearrange("p (c i) j -> p c j i", i=4), w_raw[:].rearrange("p (j c i) -> p c j i", j=PACK, i=4)
+            w_woven[:, cut:N, :].rearrange("p (c i) j -> p c j i", i=4),
+            w_rows[:, :, cut:N].rearrange("p j (c i) -> p c j i", i=4),
         )
         nc.scalar.copy(woven_s[:, :, 1:PACK], stage[:, :, piece(0)].rearrange("p j n -> p n j"))
         nc.vector.quantize_mx(out=w_codes[:].bitcast(FP8X4), scales=w_scales[:], in_=w_woven[:].rearrange("p m j -> p (m j)"))

@@ -63,17 +63,17 @@ def tile_picked_huber_none_e_kernel(tc, xT, w1, bound, offs, cen, pos1, pos2, ou
 
         nc.scalar.copy(rounded[:], plane[0][:])
         nc.scalar.activation(
-            woven_s[:, :, 0], rounded[:].indirect(offs_t[:, 0 : PIECE // PER_COL]), mybir.ActivationFunctionType.Copy
+            woven_s[:, :, 0], rounded[:].indirect(offs_t[:, 3 * PIECE // PER_COL :]), mybir.ActivationFunctionType.Copy
         )
-        nc.vector.tensor_copy(woven_v[:, :, 0], picked(0, 1, 3))
+        nc.vector.tensor_copy(woven_v[:, :, 0], picked(0, 0, 3))
         nc.vector.tensor_copy(stage[:, 1, 0:S], picked(2, 0, PIECES))
-        for s in range(1, PIECES):
-            nc.vector.tensor_copy(stage[:, 2, piece(s)], picked(3, s))
-            nc.scalar.copy(woven_v[:, piece(s - 1), 2:PACK], stage[:, 1:3, piece(s)].rearrange("p j n -> p n j"))
-        nc.vector.tensor_copy(stage[:, 2, piece(0)], picked(3, 0))
-        nc.vector.tensor_copy(woven_v[:, piece(0, 2), 1], picked(1, 1, 2))
-        nc.vector.tensor_copy(stage[:, 0, piece(0)], picked(1, 0))
-        nc.vector.tensor_copy(woven_v[:, piece(2), 1], picked(1, 3))
+        for s, count in ((0, 1), (1, 1), (2, 2)):
+            nc.vector.tensor_copy(stage[:, 2, piece(s, count)], picked(3, s, count))
+        for s in range(PIECES - 1):
+            nc.scalar.copy(woven_v[:, piece(s), 2:PACK], stage[:, 1:3, piece(s)].rearrange("p j n -> p n j"))
+        nc.vector.tensor_copy(woven_v[:, piece(0, 2), 1], picked(1, 0, 2))
+        nc.vector.tensor_copy(stage[:, 0, piece(3)], picked(1, 3))
+        nc.vector.tensor_copy(woven_v[:, piece(2), 1], picked(1, 2))
 
         w_woven = sb.tile([P, N, PACK], BF16, name="w_woven", align_bytes=64)
         w_codes = sb.tile([P, N], U32, name="w_codes", align_bytes=64)
@@ -87,17 +87,17 @@ def tile_picked_huber_none_e_kernel(tc, xT, w1, bound, offs, cen, pos1, pos2, ou
             w_woven[:, cut:N, :].rearrange("p (c i) j -> p c j i", i=4),
             w_rows[:, :, cut:N].rearrange("p j (c i) -> p c j i", i=4),
         )
-        nc.scalar.copy(woven_s[:, :, 1:PACK], stage[:, :, piece(0)].rearrange("p j n -> p n j"))
+        nc.scalar.copy(woven_s[:, :, 1:PACK], stage[:, :, piece(3)].rearrange("p j n -> p n j"))
         nc.vector.quantize_mx(out=w_codes[:].bitcast(FP8X4), scales=w_scales[:], in_=w_woven[:].rearrange("p m j -> p (m j)"))
 
         y = sb.tile([P, S], F32, name="y")
         small = PIECE // 2
         groups = [
-            (woven_v[:, piece(0), :], PIECE, PIECE),
-            (woven_v[:, piece(1), :], 2 * PIECE, PIECE),
-            (woven_v[:, piece(2), :], 3 * PIECE, PIECE),
-            (woven_s[:, 0:small, :], 0, small),
-            (woven_s[:, small:PIECE, :], small, small),
+            (woven_v[:, piece(0), :], 0, PIECE),
+            (woven_v[:, piece(1), :], PIECE, PIECE),
+            (woven_v[:, piece(2), :], 2 * PIECE, PIECE),
+            (woven_s[:, 0:small, :], 3 * PIECE, small),
+            (woven_s[:, small:PIECE, :], 3 * PIECE + small, small),
         ]
         for g, (source, first, width) in enumerate(groups):
             if g == 0:

@@ -139,25 +139,28 @@ def tile_picked_huber_none_e_kernel(tc, xT, w1, bound, offs, cen, pos1, pos2, ou
         def fetch(dst, lst, other, op, h):
             nc.vector.tensor_tensor(dst[h][:], y[:].indirect(targets(lst, h)), other, op)
 
-        def clip(dst, src, h):
-            nc.vector.scalar_tensor_tensor(dst[h][:], src[h][:], 0.0, floor[:, cols[h]], ALU.min, ALU.max)
+        def clip(dst, src, h, c=slice(0, part)):
+            nc.vector.scalar_tensor_tensor(dst[h][:, c], src[h][:, c], 0.0, floor[:, cols[h]][:, c], ALU.min, ALU.max)
 
-        def add_half(dst, pull, base, h):
-            nc.vector.scalar_tensor_tensor(dst[h][:], pull[h][:], 0.5, base[h][:], ALU.mult, ALU.add)
+        def add_half(dst, pull, base, h, c=slice(0, part)):
+            nc.vector.scalar_tensor_tensor(dst[h][:, c], pull[h][:, c], 0.5, base[h][:, c], ALU.mult, ALU.add)
 
+        quarters = [slice(0, part // 2), slice(part // 2, part)]
         for h in range(2):
             fetch(upper, cen_t, b_t[:, cols[h]], ALU.add, h)
         for h in range(2):
             fetch(excess1, pos1_t, upper[h][:], ALU.subtract, h)
-        clip(pull1, excess1, 0)
         fetch(excess2, pos2_t, upper[0][:], ALU.subtract, 0)
-        clip(pull1, excess1, 1)
-        add_half(partial, pull1, upper, 0)
+        for h in range(2):
+            clip(pull1, excess1, h)
         fetch(excess2, pos2_t, upper[1][:], ALU.subtract, 1)
         clip(pull2, excess2, 0)
-        add_half(partial, pull1, upper, 1)
-        clip(pull2, excess2, 1)
-        queues = [nc.sync, nc.sync]
         for h in range(2):
-            add_half(result, pull2, partial, h)
-            queues[h].dma_start(out[:, cols[h]], result[h][:])
+            add_half(partial, pull1, upper, h)
+        for c in quarters:
+            clip(pull2, excess2, 1, c)
+        add_half(result, pull2, partial, 0)
+        nc.sync.dma_start(out[:, cols[0]], result[0][:])
+        for c in quarters:
+            add_half(result, pull2, partial, 1, c)
+        nc.sync.dma_start(out[:, cols[1]], result[1][:])

@@ -17,8 +17,11 @@ P = 128
 PACK = 4
 PIECE = 128
 PIECES = S // PIECE
-HALF = S // 2
+LAST = PIECES - 1
 PER_COL = 16
+W_GPSIMD = 56
+W_AT = 0
+LAST_AT = W_AT + 4 * PACK * N
 
 
 def tile_picked_huber_none_e_kernel(tc, xT, w1, bound, offs, cen, pos1, pos2, out):
@@ -36,8 +39,7 @@ def tile_picked_huber_none_e_kernel(tc, xT, w1, bound, offs, cen, pos1, pos2, ou
 
         x_rows = xT.rearrange("(p j) t -> p j t", j=PACK)
         plane = [sb.tile([P, T], F32, name=f"plane{j}") for j in range(PACK)]
-        w_at, last_at = 0, 2048
-        w_raw = reuse.tile([P, PACK * N], F32, name="w_raw", align_bytes=64, offset=w_at)
+        w_raw = reuse.tile([P, PACK * N], F32, name="w_raw", align_bytes=64, offset=W_AT)
         stage = sb.tile([P, PACK - 1, S + 2 * V], BF16, name="stage")
         b_t = stage[:, 0, S : S + 2 * V].bitcast(F32)
 
@@ -51,59 +53,56 @@ def tile_picked_huber_none_e_kernel(tc, xT, w1, bound, offs, cen, pos1, pos2, ou
         nc.sync.dma_start(pos1_t[:], pos1)
         nc.sync.dma_start(pos2_t[:], pos2)
 
-        def picked(j, s, count=1):
-            return plane[j][:].indirect(offs_t[:, s * PIECE // PER_COL : (s + count) * PIECE // PER_COL])
-
-        woven_s = reuse.tile([P, PIECE, PACK], BF16, name="woven_s", align_bytes=64, offset=last_at)
-        woven_v = sb.tile([P, S - PIECE, PACK], BF16, name="woven_v", align_bytes=64)
-        rounded = sb.tile([P, T], BF16, name="rounded")
-
         def piece(s, count=1):
             return slice(s * PIECE, (s + count) * PIECE)
 
+        def entries(lst, nodes):
+            return lst[:, nodes.start // PER_COL : nodes.stop // PER_COL]
+
+        def picked(j, s, count=1):
+            return plane[j][:].indirect(entries(offs_t, piece(s, count)))
+
+        woven_s = reuse.tile([P, PIECE, PACK], BF16, name="woven_s", align_bytes=64, offset=LAST_AT)
+        woven_v = sb.tile([P, S - PIECE, PACK], BF16, name="woven_v", align_bytes=64)
+        rounded = sb.tile([P, T], BF16, name="rounded")
+
         nc.scalar.copy(rounded[:], plane[0][:])
         nc.scalar.activation(
-            woven_s[:, :, 0], rounded[:].indirect(offs_t[:, 3 * PIECE // PER_COL :]), mybir.ActivationFunctionType.Copy
+            woven_s[:, :, 0], rounded[:].indirect(entries(offs_t, piece(LAST))), mybir.ActivationFunctionType.Copy
         )
-        nc.vector.tensor_copy(woven_v[:, :, 0], picked(0, 0, 3))
+        nc.vector.tensor_copy(woven_v[:, :, 0], picked(0, 0, LAST))
         nc.vector.tensor_copy(stage[:, 1, 0:S], picked(2, 0, PIECES))
         for s, count in ((0, 1), (1, 1), (2, 2)):
             nc.vector.tensor_copy(stage[:, 2, piece(s, count)], picked(3, s, count))
-        for s in range(PIECES - 1):
+        for s in range(LAST):
             nc.scalar.copy(woven_v[:, piece(s), 2:PACK], stage[:, 1:3, piece(s)].rearrange("p j n -> p n j"))
         nc.vector.tensor_copy(woven_v[:, piece(0, 2), 1], picked(1, 0, 2))
-        nc.vector.tensor_copy(stage[:, 0, piece(3)], picked(1, 3))
+        nc.vector.tensor_copy(stage[:, 0, piece(LAST)], picked(1, LAST))
         nc.vector.tensor_copy(woven_v[:, piece(2), 1], picked(1, 2))
 
         w_woven = sb.tile([P, N, PACK], BF16, name="w_woven", align_bytes=64)
         w_codes = sb.tile([P, N], U32, name="w_codes", align_bytes=64)
         w_scales = sb.tile([P, N], U8, name="w_scales", align_bytes=64)
-        cut = 64
         w_rows = w_raw[:].rearrange("p (j m) -> p j m", j=PACK)
         nc.gpsimd.tensor_scalar(
-            w_woven[:, 0:cut, :], w_rows[:, :, 0:cut].rearrange("p j m -> p m j"), 1.0, 0.0, ALU.mult, ALU.add
+            w_woven[:, 0:W_GPSIMD, :], w_rows[:, :, 0:W_GPSIMD].rearrange("p j m -> p m j"), 1.0, 0.0, ALU.mult, ALU.add
         )
         nc.scalar.copy(
-            w_woven[:, cut:N, :].rearrange("p (c i) j -> p c j i", i=4),
-            w_rows[:, :, cut:N].rearrange("p j (c i) -> p c j i", i=4),
+            w_woven[:, W_GPSIMD:N, :].rearrange("p (c i) j -> p c j i", i=4),
+            w_rows[:, :, W_GPSIMD:N].rearrange("p j (c i) -> p c j i", i=4),
         )
-        nc.scalar.copy(woven_s[:, :, 1:PACK], stage[:, :, piece(3)].rearrange("p j n -> p n j"))
+        nc.scalar.copy(woven_s[:, :, 1:PACK], stage[:, :, piece(LAST)].rearrange("p j n -> p n j"))
         nc.vector.quantize_mx(out=w_codes[:].bitcast(FP8X4), scales=w_scales[:], in_=w_woven[:].rearrange("p m j -> p (m j)"))
 
         y = sb.tile([P, S], F32, name="y")
-        small = PIECE // 2
-        groups = [
-            (woven_v[:, piece(0), :], 0, PIECE),
-            (woven_v[:, piece(1), :], PIECE, PIECE),
-            (woven_v[:, piece(2), :], 2 * PIECE, PIECE),
-            (woven_s[:, 0:small, :], 3 * PIECE, small),
-            (woven_s[:, small:PIECE, :], 3 * PIECE + small, small),
-        ]
+        narrow = PIECE // 2
+        groups = [(woven_v[:, piece(s), :], s * PIECE, PIECE) for s in range(LAST)]
+        groups = groups + [(woven_s[:, at : at + narrow, :], LAST * PIECE + at, narrow) for at in (0, narrow)]
         for g, (source, first, width) in enumerate(groups):
             if g == 0:
                 codes = sb.tile([P, width], U32, name=f"codes{g}", align_bytes=64)
             else:
-                codes = reuse.tile([P, width], U32, name=f"codes{g}", align_bytes=64, offset=w_at + 4 * first)
+                codes = reuse.tile([P, width], U32, name=f"codes{g}", align_bytes=64, offset=W_AT + 4 * first)
             scales = sb.tile([P, width], U8, name=f"scales{g}", align_bytes=64)
             nc.vector.quantize_mx(out=codes[:].bitcast(FP8X4), scales=scales[:], in_=source.rearrange("p n j -> p (n j)"))
             acc = ps.tile([P, width], F32, name=f"acc{g}")
@@ -116,19 +115,16 @@ def tile_picked_huber_none_e_kernel(tc, xT, w1, bound, offs, cen, pos1, pos2, ou
                 start=True,
                 stop=True,
             )
-            if g == len(groups) - 1:
+            if g == len(groups) - 2:
                 nc.vector.tensor_copy(y[:, first : first + width], acc[:])
             else:
                 nc.scalar.copy(y[:, first : first + width], acc[:])
 
-        floor = reuse.tile([P, V], F32, name="floor", align_bytes=64, offset=last_at)
+        floor = reuse.tile([P, V], F32, name="floor", align_bytes=64, offset=LAST_AT)
         nc.vector.tensor_scalar(floor[:], b_t, -2.0, None, ALU.mult)
 
         part = V // 2
         cols = [slice(0, part), slice(part, V)]
-
-        def targets(lst, h):
-            return lst[:, h * part // PER_COL : (h + 1) * part // PER_COL]
 
         def halves(name):
             return [sb.tile([P, part], F32, name=f"{name}{h}") for h in range(2)]
@@ -137,7 +133,7 @@ def tile_picked_huber_none_e_kernel(tc, xT, w1, bound, offs, cen, pos1, pos2, ou
         pull1, pull2, partial, result = halves("pull1"), halves("pull2"), halves("partial"), halves("result")
 
         def fetch(dst, lst, other, op, h):
-            nc.vector.tensor_tensor(dst[h][:], y[:].indirect(targets(lst, h)), other, op)
+            nc.vector.tensor_tensor(dst[h][:], y[:].indirect(entries(lst, cols[h])), other, op)
 
         def clip(dst, src, h, c=slice(0, part)):
             nc.vector.scalar_tensor_tensor(dst[h][:, c], src[h][:, c], 0.0, floor[:, cols[h]][:, c], ALU.min, ALU.max)
@@ -145,7 +141,6 @@ def tile_picked_huber_none_e_kernel(tc, xT, w1, bound, offs, cen, pos1, pos2, ou
         def add_half(dst, pull, base, h, c=slice(0, part)):
             nc.vector.scalar_tensor_tensor(dst[h][:, c], pull[h][:, c], 0.5, base[h][:, c], ALU.mult, ALU.add)
 
-        quarters = [slice(0, part // 2), slice(part // 2, part)]
         for h in range(2):
             fetch(upper, cen_t, b_t[:, cols[h]], ALU.add, h)
         for h in range(2):
@@ -157,6 +152,7 @@ def tile_picked_huber_none_e_kernel(tc, xT, w1, bound, offs, cen, pos1, pos2, ou
         clip(pull2, excess2, 0)
         for h in range(2):
             add_half(partial, pull1, upper, h)
+        quarters = [slice(0, part // 2), slice(part // 2, part)]
         for c in quarters:
             clip(pull2, excess2, 1, c)
         add_half(result, pull2, partial, 0)

@@ -1,6 +1,7 @@
 from contextlib import ExitStack
 
 import concourse.mybir as mybir
+from concourse.masks import make_identity
 
 K, T, S, V, N = 512, 1024, 512, 256, 128
 FLOPS = 2 * K * N * S
@@ -12,6 +13,7 @@ U16 = mybir.dt.uint16
 U8 = mybir.dt.uint8
 FP8X4 = mybir.dt.float8_e4m3fn_x4
 ALU = mybir.AluOpType
+ACT = mybir.ActivationFunctionType
 
 P = 128
 PACK = 4
@@ -105,7 +107,7 @@ def tile_picked_huber_none_e_kernel(tc, xT, w1, bound, offs, cen, pos1, pos2, ou
                 codes = reuse.tile([P, width], U32, name=f"codes{g}", align_bytes=64, offset=W_AT + 4 * first)
             scales = sb.tile([P, width], U8, name=f"scales{g}", align_bytes=64)
             nc.vector.quantize_mx(out=codes[:].bitcast(FP8X4), scales=scales[:], in_=source.rearrange("p n j -> p (n j)"))
-            acc = ps.tile([P, width], F32, name=f"acc{g}")
+            acc = ps.tile([P, width], F32, name=f"acc{g}", tag=f"bank{g}")
             nc.tensor.matmul_mx(
                 out=acc[:],
                 lhsT=w_codes[:].bitcast(FP8X4),
@@ -120,43 +122,62 @@ def tile_picked_huber_none_e_kernel(tc, xT, w1, bound, offs, cen, pos1, pos2, ou
             else:
                 nc.scalar.copy(y[:, first : first + width], acc[:])
 
-        floor = reuse.tile([P, V], F32, name="floor", align_bytes=64, offset=LAST_AT)
-        nc.vector.tensor_scalar(floor[:], b_t, -2.0, None, ALU.mult)
-
         part = V // 2
-        cols = [slice(0, part), slice(part, V)]
+        first_half, second_half = slice(0, part), slice(part, V)
 
-        def halves(name):
-            return [sb.tile([P, part], F32, name=f"{name}{h}") for h in range(2)]
+        def fetch(name, lst, cols, other, op):
+            dst = sb.tile([P, part], F32, name=name)
+            nc.vector.tensor_tensor(dst[:], y[:].indirect(entries(lst, cols)), other, op)
+            return dst
 
-        upper, excess1, excess2 = halves("upper"), halves("excess1"), halves("excess2")
-        pull1, pull2, partial, result = halves("pull1"), halves("pull2"), halves("partial"), halves("result")
+        ident = sb.tile([P, P], F32, name="ident")
+        make_identity(nc, ident[:])
+        minus_one = sb.tile([P, part], F32, name="minus_one")
+        nc.gpsimd.memset(minus_one[:], -1.0)
 
-        def fetch(dst, lst, other, op, h):
-            nc.vector.tensor_tensor(dst[h][:], y[:].indirect(entries(lst, cols[h])), other, op)
+        def turn(name, bank, *sources):
+            dst = ps.tile([P, P], F32, name=name, tag=f"bank{bank}")
+            for i, src in enumerate(sources):
+                nc.tensor.matmul(dst[:], src, ident[:], start=(i == 0), stop=(i == len(sources) - 1), is_transpose=True)
+            return dst
 
-        def clip(dst, src, h, c=slice(0, part)):
-            nc.vector.scalar_tensor_tensor(dst[h][:, c], src[h][:, c], 0.0, floor[:, cols[h]][:, c], ALU.min, ALU.max)
+        b_col = sb.tile([P, 1], F32, name="b_col")
+        nc.scalar.copy(b_col[:], turn("b_turned", len(groups) - 1, b_t[:, first_half])[:, 0:1])
 
-        def add_half(dst, pull, base, h, c=slice(0, part)):
-            nc.vector.scalar_tensor_tensor(dst[h][:, c], pull[h][:, c], 0.5, base[h][:, c], ALU.mult, ALU.add)
+        lower_a = fetch("lower_a", cen_t, first_half, b_t[:, first_half], ALU.subtract)
+        minus_y1 = fetch("minus_y1", pos1_t, first_half, minus_one[:], ALU.mult)
+        lower_b = fetch("lower_b", cen_t, second_half, b_t[:, second_half], ALU.subtract)
+        rise2_a = fetch("rise2_a", pos2_t, first_half, lower_a[:], ALU.subtract)
+        rise1_b = fetch("rise1_b", pos1_t, second_half, lower_b[:], ALU.subtract)
+        rise2_b = fetch("rise2_b", pos2_t, second_half, lower_b[:], ALU.subtract)
 
-        for h in range(2):
-            fetch(upper, cen_t, b_t[:, cols[h]], ALU.add, h)
-        for h in range(2):
-            fetch(excess1, pos1_t, upper[h][:], ALU.subtract, h)
-        fetch(excess2, pos2_t, upper[0][:], ALU.subtract, 0)
-        for h in range(2):
-            clip(pull1, excess1, h)
-        fetch(excess2, pos2_t, upper[1][:], ALU.subtract, 1)
-        clip(pull2, excess2, 0)
-        for h in range(2):
-            add_half(partial, pull1, upper, h)
-        quarters = [slice(0, part // 2), slice(part // 2, part)]
-        for c in quarters:
-            clip(pull2, excess2, 1, c)
-        add_half(result, pull2, partial, 0)
-        nc.sync.dma_start(out[:, cols[0]], result[0][:])
-        for c in quarters:
-            add_half(result, pull2, partial, 1, c)
-        nc.sync.dma_start(out[:, cols[1]], result[1][:])
+        fall = turn("fall", 0, lower_a[:], minus_y1[:])
+        lower_turned = sb.tile([P, P], F32, name="lower_turned")
+        nc.scalar.copy(lower_turned[:], turn("lower_in_bank", 1, lower_a[:])[:])
+        room = sb.tile([P, P], F32, name="room")
+        share = sb.tile([P, P], F32, name="share")
+        features = [slice(0, P // 2), slice(P // 2, P)]
+        for c in features:
+            nc.scalar.activation(room[:, c], fall[:, c], ACT.Relu, bias=b_col[:], scale=0.5)
+        for c in features:
+            nc.scalar.activation(share[:, c], room[:, c], ACT.Relu, bias=b_col[:], scale=-1.0)
+        partial_a = turn("partial_a", 2, lower_turned[:], share[:])
+
+        def cap(name, rise, cols):
+            dst = sb.tile([P, part], F32, name=name)
+            nc.vector.scalar_tensor_tensor(dst[:], rise[:], 0.5, b_t[:, cols], ALU.mult, ALU.min)
+            return dst
+
+        def add_share(name, capped, base):
+            dst = sb.tile([P, part], F32, name=name)
+            nc.vector.scalar_tensor_tensor(dst[:], capped[:], 0.0, base[:], ALU.max, ALU.add)
+            return dst
+
+        capped1_b = cap("capped1_b", rise1_b, second_half)
+        capped2_b = cap("capped2_b", rise2_b, second_half)
+        partial_b = add_share("partial_b", capped1_b, lower_b)
+        capped2_a = cap("capped2_a", rise2_a, first_half)
+        result_b = add_share("result_b", capped2_b, partial_b)
+        nc.sync.dma_start(out[:, second_half], result_b[:])
+        result_a = add_share("result_a", capped2_a, partial_a)
+        nc.sync.dma_start(out[:, first_half], result_a[:])

@@ -163,21 +163,25 @@ def tile_picked_huber_none_e_kernel(tc, xT, w1, bound, offs, cen, pos1, pos2, ou
             nc.scalar.activation(share[:, c], room[:, c], ACT.Relu, bias=b_col[:], scale=-1.0)
         partial_a = turn("partial_a", 2, lower_turned[:], share[:])
 
-        def cap(name, rise, cols):
-            dst = sb.tile([P, part], F32, name=name)
-            nc.vector.scalar_tensor_tensor(dst[:], rise[:], 0.5, b_t[:, cols], ALU.mult, ALU.min)
-            return dst
+        whole = slice(0, part)
+        quarters = [slice(0, part // 2), slice(part // 2, part)]
 
-        def add_share(name, capped, base):
-            dst = sb.tile([P, part], F32, name=name)
-            nc.vector.scalar_tensor_tensor(dst[:], capped[:], 0.0, base[:], ALU.max, ALU.add)
-            return dst
+        def cap(dst, rise, cols, c=whole):
+            nc.vector.scalar_tensor_tensor(dst[:, c], rise[:, c], 0.5, b_t[:, cols][:, c], ALU.mult, ALU.min)
 
-        capped1_b = cap("capped1_b", rise1_b, second_half)
-        capped2_b = cap("capped2_b", rise2_b, second_half)
-        partial_b = add_share("partial_b", capped1_b, lower_b)
-        capped2_a = cap("capped2_a", rise2_a, first_half)
-        result_b = add_share("result_b", capped2_b, partial_b)
-        nc.sync.dma_start(out[:, second_half], result_b[:])
-        result_a = add_share("result_a", capped2_a, partial_a)
+        def add_share(dst, capped, base, c=whole):
+            nc.vector.scalar_tensor_tensor(dst[:, c], capped[:, c], 0.0, base[:, c], ALU.max, ALU.add)
+
+        names = ("capped1_b", "capped2_a", "capped2_b", "partial_b", "result_a", "result_b")
+        capped1_b, capped2_a, capped2_b, partial_b, result_a, result_b = [sb.tile([P, part], F32, name=n) for n in names]
+        for c in quarters:
+            cap(capped1_b, rise1_b, second_half, c)
+        cap(capped2_a, rise2_a, first_half)
+        for c in quarters:
+            cap(capped2_b, rise2_b, second_half, c)
+            add_share(partial_b, capped1_b, lower_b, c)
+        add_share(result_b, capped2_b, partial_b, quarters[0])
+        add_share(result_a, capped2_a, partial_a)
         nc.sync.dma_start(out[:, first_half], result_a[:])
+        add_share(result_b, capped2_b, partial_b, quarters[1])
+        nc.sync.dma_start(out[:, second_half], result_b[:])

@@ -142,16 +142,16 @@ def tile_picked_huber_none_e_kernel(tc, xT, w1, bound, offs, cen, pos1, pos2, ou
             return dst
 
         b_col = sb.tile([P, 1], F32, name="b_col")
-        nc.scalar.copy(b_col[:], turn("b_turned", len(groups) - 1, b_t[:, first_half])[:, 0:1])
+        nc.scalar.copy(b_col[:], turn("b_turned", len(groups) - 2, b_t[:, first_half])[:, 0:1])
 
-        lower_a = fetch("lower_a", cen_t, first_half, b_t[:, first_half], ALU.subtract)
         minus_y1 = fetch("minus_y1", pos1_t, first_half, minus_one[:], ALU.mult)
+        lower_a = fetch("lower_a", cen_t, first_half, b_t[:, first_half], ALU.subtract)
         lower_b = fetch("lower_b", cen_t, second_half, b_t[:, second_half], ALU.subtract)
         rise2_a = fetch("rise2_a", pos2_t, first_half, lower_a[:], ALU.subtract)
         rise1_b = fetch("rise1_b", pos1_t, second_half, lower_b[:], ALU.subtract)
         rise2_b = fetch("rise2_b", pos2_t, second_half, lower_b[:], ALU.subtract)
 
-        fall = turn("fall", 0, lower_a[:], minus_y1[:])
+        fall = turn("fall", 0, minus_y1[:], lower_a[:])
         lower_turned = sb.tile([P, P], F32, name="lower_turned")
         nc.scalar.copy(lower_turned[:], turn("lower_in_bank", 1, lower_a[:])[:])
         room = sb.tile([P, P], F32, name="room")

@@ -1,7 +1,6 @@
 from contextlib import ExitStack
 
 import concourse.mybir as mybir
-from concourse.masks import make_identity
 
 K, T, S, V, N = 512, 1024, 512, 256, 128
 FLOPS = 2 * K * N * S
@@ -17,13 +16,11 @@ ACT = mybir.ActivationFunctionType
 
 P = 128
 PACK = 4
-PIECE = 128
-PIECES = S // PIECE
-LAST = PIECES - 1
 PER_COL = 16
+WIDE = 128
+NARROW = 64
+NODES_V = 320
 W_GPSIMD = 56
-W_AT = 0
-LAST_AT = W_AT + 4 * PACK * N
 
 
 def tile_picked_huber_none_e_kernel(tc, xT, w1, bound, offs, cen, pos1, pos2, out):
@@ -40,47 +37,46 @@ def tile_picked_huber_none_e_kernel(tc, xT, w1, bound, offs, cen, pos1, pos2, ou
         pos2_t = lists.tile([P, V // PER_COL], U16, name="pos2_t")
 
         x_rows = xT.rearrange("(p j) t -> p j t", j=PACK)
-        plane = [sb.tile([P, T], F32, name=f"plane{j}") for j in range(PACK)]
-        w_raw = reuse.tile([P, PACK * N], F32, name="w_raw", align_bytes=64, offset=W_AT)
-        stage = sb.tile([P, PACK - 1, S + 2 * V], BF16, name="stage")
-        b_t = stage[:, 0, S : S + 2 * V].bitcast(F32)
+        plane = [sb.tile([P, T], F32, name=f"plane{j}", align_bytes=256) for j in range(PACK)]
+        w_raw = reuse.tile([P, PACK * N], F32, name="w_raw", align_bytes=256, offset=0)
+        b_t = sb.tile([P, V], F32, name="b_t", align_bytes=256)
 
         nc.sync.dma_start(plane[0][:], x_rows[:, 0, :])
         nc.sync.dma_start(offs_t[:], offs)
-        for j in (2, 3, 1):
+        for j in range(1, PACK):
             nc.sync.dma_start(plane[j][:], x_rows[:, j, :])
         nc.sync.dma_start(w_raw[:], w1.rearrange("(p j) m -> p (j m)", j=PACK))
-        nc.sync.dma_start(b_t, bound)
+        nc.sync.dma_start(b_t[:], bound)
         nc.sync.dma_start(cen_t[:], cen)
         nc.sync.dma_start(pos1_t[:], pos1)
         nc.sync.dma_start(pos2_t[:], pos2)
 
-        def piece(s, count=1):
-            return slice(s * PIECE, (s + count) * PIECE)
+        ones = sb.tile([P, 1], F32, name="ones")
+        halves = sb.tile([P, 1], F32, name="halves")
+        nc.vector.memset(ones[:], 1.0)
+        nc.scalar.activation(halves[:], ones[:], ACT.Copy, scale=0.5)
 
-        def entries(lst, nodes):
-            return lst[:, nodes.start // PER_COL : nodes.stop // PER_COL]
+        def entries(lst, first, count):
+            return lst[:, first // PER_COL : (first + count) // PER_COL]
 
-        def picked(j, s, count=1):
-            return plane[j][:].indirect(entries(offs_t, piece(s, count)))
+        woven_v = sb.tile([P, NODES_V, PACK], BF16, name="woven_v", align_bytes=64)
+        woven_s = sb.tile([P, S - NODES_V, PACK], BF16, name="woven_s", align_bytes=64)
 
-        woven_s = reuse.tile([P, PIECE, PACK], BF16, name="woven_s", align_bytes=64, offset=LAST_AT)
-        woven_v = sb.tile([P, S - PIECE, PACK], BF16, name="woven_v", align_bytes=64)
-        rounded = sb.tile([P, T], BF16, name="rounded")
+        def place_v(j, first, count):
+            nc.vector.tensor_copy(woven_v[:, first : first + count, j], plane[j][:].indirect(entries(offs_t, first, count)))
 
-        nc.scalar.copy(rounded[:], plane[0][:])
-        nc.scalar.activation(
-            woven_s[:, :, 0], rounded[:].indirect(entries(offs_t, piece(LAST))), mybir.ActivationFunctionType.Copy
-        )
-        nc.vector.tensor_copy(woven_v[:, :, 0], picked(0, 0, LAST))
-        nc.vector.tensor_copy(stage[:, 1, 0:S], picked(2, 0, PIECES))
-        for s, count in ((0, 1), (1, 1), (2, 2)):
-            nc.vector.tensor_copy(stage[:, 2, piece(s, count)], picked(3, s, count))
-        for s in range(LAST):
-            nc.scalar.copy(woven_v[:, piece(s), 2:PACK], stage[:, 1:3, piece(s)].rearrange("p j n -> p n j"))
-        nc.vector.tensor_copy(woven_v[:, piece(0, 2), 1], picked(1, 0, 2))
-        nc.vector.tensor_copy(stage[:, 0, piece(LAST)], picked(1, LAST))
-        nc.vector.tensor_copy(woven_v[:, piece(2), 1], picked(1, 2))
+        def place_s(j, first, count):
+            nc.scalar.activation(
+                woven_s[:, first : first + count, j], plane[j][:].indirect(entries(offs_t, NODES_V + first, count)), ACT.Copy
+            )
+
+        for j in range(PACK - 1):
+            place_v(j, 0, NODES_V)
+            place_s(j, 0, S - NODES_V)
+        place_v(PACK - 1, 0, WIDE)
+        place_v(PACK - 1, WIDE, NODES_V - WIDE)
+        place_s(PACK - 1, 0, WIDE)
+        place_s(PACK - 1, WIDE, NARROW)
 
         w_woven = sb.tile([P, N, PACK], BF16, name="w_woven", align_bytes=64)
         w_codes = sb.tile([P, N], U32, name="w_codes", align_bytes=64)
@@ -93,18 +89,21 @@ def tile_picked_huber_none_e_kernel(tc, xT, w1, bound, offs, cen, pos1, pos2, ou
             w_woven[:, W_GPSIMD:N, :].rearrange("p (c i) j -> p c j i", i=4),
             w_rows[:, :, W_GPSIMD:N].rearrange("p j (c i) -> p c j i", i=4),
         )
-        nc.scalar.copy(woven_s[:, :, 1:PACK], stage[:, :, piece(LAST)].rearrange("p j n -> p n j"))
         nc.vector.quantize_mx(out=w_codes[:].bitcast(FP8X4), scales=w_scales[:], in_=w_woven[:].rearrange("p m j -> p (m j)"))
 
         y = sb.tile([P, S], F32, name="y")
-        narrow = PIECE // 2
-        groups = [(woven_v[:, piece(s), :], s * PIECE, PIECE) for s in range(LAST)]
-        groups = groups + [(woven_s[:, at : at + narrow, :], LAST * PIECE + at, narrow) for at in (0, narrow)]
+        groups = [
+            (woven_s[:, 0:WIDE, :], NODES_V, WIDE),
+            (woven_v[:, 0:WIDE, :], 0, WIDE),
+            (woven_v[:, WIDE : 2 * WIDE, :], WIDE, WIDE),
+            (woven_v[:, 2 * WIDE : NODES_V, :], 2 * WIDE, NARROW),
+            (woven_s[:, WIDE : WIDE + NARROW, :], NODES_V + WIDE, NARROW),
+        ]
         for g, (source, first, width) in enumerate(groups):
             if g == 0:
                 codes = sb.tile([P, width], U32, name=f"codes{g}", align_bytes=64)
             else:
-                codes = reuse.tile([P, width], U32, name=f"codes{g}", align_bytes=64, offset=W_AT + 4 * first)
+                codes = reuse.tile([P, width], U32, name=f"codes{g}", align_bytes=256, offset=4 * first)
             scales = sb.tile([P, width], U8, name=f"scales{g}", align_bytes=64)
             nc.vector.quantize_mx(out=codes[:].bitcast(FP8X4), scales=scales[:], in_=source.rearrange("p n j -> p (n j)"))
             acc = ps.tile([P, width], F32, name=f"acc{g}", tag=f"bank{g}")
@@ -122,66 +121,41 @@ def tile_picked_huber_none_e_kernel(tc, xT, w1, bound, offs, cen, pos1, pos2, ou
             else:
                 nc.scalar.copy(y[:, first : first + width], acc[:])
 
-        part = V // 2
-        first_half, second_half = slice(0, part), slice(part, V)
+        half = V // 2
+        lower = sb.tile([P, V], F32, name="lower")
+        near = [sb.tile([P, 2, half], F32, name=f"near{h}") for h in range(2)]
+        rise = [sb.tile([P, 2, half], F32, name=f"rise{h}") for h in range(2)]
+        capped = [sb.tile([P, 2, half], F32, name=f"capped{h}") for h in range(2)]
+        partial = [sb.tile([P, half], F32, name=f"partial{h}") for h in range(2)]
+        result = [sb.tile([P, half], F32, name=f"result{h}") for h in range(2)]
+        cols = [slice(0, half), slice(half, V)]
 
-        def fetch(name, lst, cols, other, op):
-            dst = sb.tile([P, part], F32, name=name)
-            nc.vector.tensor_tensor(dst[:], y[:].indirect(entries(lst, cols)), other, op)
-            return dst
+        for h in range(2):
+            nc.vector.tensor_tensor(lower[:, cols[h]], y[:].indirect(entries(cen_t, h * half, half)), b_t[:, cols[h]], ALU.subtract)
+            for d, lst in enumerate((pos1_t, pos2_t)):
+                nc.scalar.activation(near[h][:, d, :], y[:].indirect(entries(lst, h * half, half)), ACT.Copy, scale=halves[:])
 
-        ident = sb.tile([P, P], F32, name="ident")
-        make_identity(nc, ident[:])
-        minus_one = sb.tile([P, part], F32, name="minus_one")
-        nc.gpsimd.memset(minus_one[:], -1.0)
+        def both(ap):
+            return ap.unsqueeze(1).to_broadcast([P, 2, half])
 
-        def turn(name, bank, *sources):
-            dst = ps.tile([P, P], F32, name=name, tag=f"bank{bank}")
-            for i, src in enumerate(sources):
-                nc.tensor.matmul(dst[:], src, ident[:], start=(i == 0), stop=(i == len(sources) - 1), is_transpose=True)
-            return dst
+        def cap(h, d):
+            nc.vector.tensor_tensor(capped[h][:, d, :], rise[h][:, d, :], b_t[:, cols[h]], ALU.min)
 
-        b_col = sb.tile([P, 1], F32, name="b_col")
-        nc.scalar.copy(b_col[:], turn("b_turned", len(groups) - 2, b_t[:, first_half])[:, 0:1])
+        def lift(dst, low, high):
+            nc.vector.scalar_tensor_tensor(dst, low, -0.5, high, ALU.mult, ALU.add)
 
-        minus_y1 = fetch("minus_y1", pos1_t, first_half, minus_one[:], ALU.mult)
-        lower_a = fetch("lower_a", cen_t, first_half, b_t[:, first_half], ALU.subtract)
-        lower_b = fetch("lower_b", cen_t, second_half, b_t[:, second_half], ALU.subtract)
-        rise2_a = fetch("rise2_a", pos2_t, first_half, lower_a[:], ALU.subtract)
-        rise1_b = fetch("rise1_b", pos1_t, second_half, lower_b[:], ALU.subtract)
-        rise2_b = fetch("rise2_b", pos2_t, second_half, lower_b[:], ALU.subtract)
+        def add_share(dst, h, d, base):
+            nc.vector.scalar_tensor_tensor(dst[:], capped[h][:, d, :], 0.0, base, ALU.max, ALU.add)
 
-        fall = turn("fall", 0, minus_y1[:], lower_a[:])
-        lower_turned = sb.tile([P, P], F32, name="lower_turned")
-        nc.scalar.copy(lower_turned[:], turn("lower_in_bank", 1, lower_a[:])[:])
-        room = sb.tile([P, P], F32, name="room")
-        share = sb.tile([P, P], F32, name="share")
-        features = [slice(0, P // 2), slice(P // 2, P)]
-        for c in features:
-            nc.scalar.activation(room[:, c], fall[:, c], ACT.Relu, bias=b_col[:], scale=0.5)
-        for c in features:
-            nc.scalar.activation(share[:, c], room[:, c], ACT.Relu, bias=b_col[:], scale=-1.0)
-        partial_a = turn("partial_a", 2, lower_turned[:], share[:])
-
-        whole = slice(0, part)
-        quarters = [slice(0, part // 2), slice(part // 2, part)]
-
-        def cap(dst, rise, cols, c=whole):
-            nc.vector.scalar_tensor_tensor(dst[:, c], rise[:, c], 0.5, b_t[:, cols][:, c], ALU.mult, ALU.min)
-
-        def add_share(dst, capped, base, c=whole):
-            nc.vector.scalar_tensor_tensor(dst[:, c], capped[:, c], 0.0, base[:, c], ALU.max, ALU.add)
-
-        names = ("capped1_b", "capped2_a", "capped2_b", "partial_b", "result_a", "result_b")
-        capped1_b, capped2_a, capped2_b, partial_b, result_a, result_b = [sb.tile([P, part], F32, name=n) for n in names]
-        for c in quarters:
-            cap(capped1_b, rise1_b, second_half, c)
-        cap(capped2_a, rise2_a, first_half)
-        for c in quarters:
-            cap(capped2_b, rise2_b, second_half, c)
-            add_share(partial_b, capped1_b, lower_b, c)
-        add_share(result_b, capped2_b, partial_b, quarters[0])
-        add_share(result_a, capped2_a, partial_a)
-        nc.sync.dma_start(out[:, first_half], result_a[:])
-        add_share(result_b, capped2_b, partial_b, quarters[1])
-        nc.sync.dma_start(out[:, second_half], result_b[:])
+        lift(rise[0][:], both(lower[:, cols[0]]), near[0][:])
+        lift(rise[1][:, 0, :], lower[:, cols[1]], near[1][:, 0, :])
+        nc.vector.tensor_tensor(capped[0][:], rise[0][:], both(b_t[:, cols[0]]), ALU.min)
+        lift(rise[1][:, 1, :], lower[:, cols[1]], near[1][:, 1, :])
+        cap(1, 0)
+        add_share(partial[0], 0, 0, lower[:, cols[0]])
+        cap(1, 1)
+        add_share(partial[1], 1, 0, lower[:, cols[1]])
+        add_share(result[0], 0, 1, partial[0][:])
+        nc.sync.dma_start(out[:, cols[0]], result[0][:])
+        add_share(result[1], 1, 1, partial[1][:])
+        nc.sync.dma_start(out[:, cols[1]], result[1][:])

@@ -20,6 +20,7 @@ PER_COL = 16
 WIDE = 128
 NARROW = 64
 NODES_V = 320
+NODES_V_EARLY = 288
 W_GPSIMD = 56
 
 
@@ -59,24 +60,21 @@ def tile_picked_huber_none_e_kernel(tc, xT, w1, bound, offs, cen, pos1, pos2, ou
         def entries(lst, first, count):
             return lst[:, first // PER_COL : (first + count) // PER_COL]
 
-        woven_v = sb.tile([P, NODES_V, PACK], BF16, name="woven_v", align_bytes=64)
-        woven_s = sb.tile([P, S - NODES_V, PACK], BF16, name="woven_s", align_bytes=64)
+        woven = sb.tile([P, S, PACK], BF16, name="woven", align_bytes=64)
 
         def place_v(j, first, count):
-            nc.vector.tensor_copy(woven_v[:, first : first + count, j], plane[j][:].indirect(entries(offs_t, first, count)))
+            nc.vector.tensor_copy(woven[:, first : first + count, j], plane[j][:].indirect(entries(offs_t, first, count)))
 
         def place_s(j, first, count):
-            nc.scalar.activation(
-                woven_s[:, first : first + count, j], plane[j][:].indirect(entries(offs_t, NODES_V + first, count)), ACT.Copy
-            )
+            nc.scalar.activation(woven[:, first : first + count, j], plane[j][:].indirect(entries(offs_t, first, count)), ACT.Copy)
 
-        for j in range(PACK - 1):
-            place_v(j, 0, NODES_V)
-            place_s(j, 0, S - NODES_V)
+        for j, split in ((0, NODES_V_EARLY), (1, NODES_V_EARLY), (2, NODES_V)):
+            place_v(j, 0, split)
+            place_s(j, split, S - split)
         place_v(PACK - 1, 0, WIDE)
         place_v(PACK - 1, WIDE, NODES_V - WIDE)
-        place_s(PACK - 1, 0, WIDE)
-        place_s(PACK - 1, WIDE, NARROW)
+        place_s(PACK - 1, NODES_V, WIDE)
+        place_s(PACK - 1, NODES_V + WIDE, NARROW)
 
         w_woven = sb.tile([P, N, PACK], BF16, name="w_woven", align_bytes=64)
         w_codes = sb.tile([P, N], U32, name="w_codes", align_bytes=64)
@@ -92,14 +90,9 @@ def tile_picked_huber_none_e_kernel(tc, xT, w1, bound, offs, cen, pos1, pos2, ou
         nc.vector.quantize_mx(out=w_codes[:].bitcast(FP8X4), scales=w_scales[:], in_=w_woven[:].rearrange("p m j -> p (m j)"))
 
         y = sb.tile([P, S], F32, name="y")
-        groups = [
-            (woven_s[:, 0:WIDE, :], NODES_V, WIDE),
-            (woven_v[:, 0:WIDE, :], 0, WIDE),
-            (woven_v[:, WIDE : 2 * WIDE, :], WIDE, WIDE),
-            (woven_v[:, 2 * WIDE : NODES_V, :], 2 * WIDE, NARROW),
-            (woven_s[:, WIDE : WIDE + NARROW, :], NODES_V + WIDE, NARROW),
-        ]
-        for g, (source, first, width) in enumerate(groups):
+        groups = [(NODES_V, WIDE), (0, WIDE), (WIDE, WIDE), (2 * WIDE, NARROW), (NODES_V + WIDE, NARROW)]
+        for g, (first, width) in enumerate(groups):
+            source = woven[:, first : first + width, :]
             if g == 0:
                 codes = sb.tile([P, width], U32, name=f"codes{g}", align_bytes=64)
             else:
@@ -122,40 +115,47 @@ def tile_picked_huber_none_e_kernel(tc, xT, w1, bound, offs, cen, pos1, pos2, ou
                 nc.scalar.copy(y[:, first : first + width], acc[:])
 
         half = V // 2
-        lower = sb.tile([P, V], F32, name="lower")
-        near = [sb.tile([P, 2, half], F32, name=f"near{h}") for h in range(2)]
-        rise = [sb.tile([P, 2, half], F32, name=f"rise{h}") for h in range(2)]
-        capped = [sb.tile([P, 2, half], F32, name=f"capped{h}") for h in range(2)]
-        partial = [sb.tile([P, half], F32, name=f"partial{h}") for h in range(2)]
-        result = [sb.tile([P, half], F32, name=f"result{h}") for h in range(2)]
         cols = [slice(0, half), slice(half, V)]
 
+        def tiles(name):
+            return [sb.tile([P, half], F32, name=f"{name}{h}") for h in range(2)]
+
+        lower, near1, rise1, rise2, capped1, capped2, partial, result = [
+            tiles(n) for n in ("lower", "near1", "rise1", "rise2", "capped1", "capped2", "partial", "result")
+        ]
+        near2_b = sb.tile([P, half], F32, name="near2_b")
+
+        def looked_up(lst, h):
+            return y[:].indirect(entries(lst, h * half, half))
+
         for h in range(2):
-            nc.vector.tensor_tensor(lower[:, cols[h]], y[:].indirect(entries(cen_t, h * half, half)), b_t[:, cols[h]], ALU.subtract)
-            for d, lst in enumerate((pos1_t, pos2_t)):
-                nc.scalar.activation(near[h][:, d, :], y[:].indirect(entries(lst, h * half, half)), ACT.Copy, scale=halves[:])
+            nc.vector.tensor_tensor(lower[h][:], looked_up(cen_t, h), b_t[:, cols[h]], ALU.subtract)
+            nc.scalar.activation(near1[h][:], looked_up(pos1_t, h), ACT.Copy, scale=halves[:])
+        nc.scalar.activation(near2_b[:], looked_up(pos2_t, 1), ACT.Copy, scale=halves[:])
+        nc.vector.tensor_tensor(rise2[0][:], looked_up(pos2_t, 0), lower[0][:], ALU.subtract)
 
-        def both(ap):
-            return ap.unsqueeze(1).to_broadcast([P, 2, half])
+        def lift(dst, near, h):
+            nc.vector.scalar_tensor_tensor(dst[:], lower[h][:], -0.5, near[:], ALU.mult, ALU.add)
 
-        def cap(h, d):
-            nc.vector.tensor_tensor(capped[h][:, d, :], rise[h][:, d, :], b_t[:, cols[h]], ALU.min)
+        def cap(dst, rise, h, factor=1.0):
+            nc.vector.scalar_tensor_tensor(dst[:], rise[:], factor, b_t[:, cols[h]], ALU.mult, ALU.min)
 
-        def lift(dst, low, high):
-            nc.vector.scalar_tensor_tensor(dst, low, -0.5, high, ALU.mult, ALU.add)
+        def add_share(dst, capped, base, c=slice(0, half)):
+            nc.vector.scalar_tensor_tensor(dst[:, c], capped[:, c], 0.0, base[:, c], ALU.max, ALU.add)
 
-        def add_share(dst, h, d, base):
-            nc.vector.scalar_tensor_tensor(dst[:], capped[h][:, d, :], 0.0, base, ALU.max, ALU.add)
-
-        lift(rise[0][:], both(lower[:, cols[0]]), near[0][:])
-        lift(rise[1][:, 0, :], lower[:, cols[1]], near[1][:, 0, :])
-        nc.vector.tensor_tensor(capped[0][:], rise[0][:], both(b_t[:, cols[0]]), ALU.min)
-        lift(rise[1][:, 1, :], lower[:, cols[1]], near[1][:, 1, :])
-        cap(1, 0)
-        add_share(partial[0], 0, 0, lower[:, cols[0]])
-        cap(1, 1)
-        add_share(partial[1], 1, 0, lower[:, cols[1]])
-        add_share(result[0], 0, 1, partial[0][:])
+        quarters = [slice(0, half // 2), slice(half // 2, half)]
+        lift(rise1[0], near1[0], 0)
+        lift(rise1[1], near1[1], 1)
+        cap(capped2[0], rise2[0], 0, 0.5)
+        cap(capped1[0], rise1[0], 0)
+        lift(rise2[1], near2_b, 1)
+        cap(capped1[1], rise1[1], 1)
+        add_share(partial[0], capped2[0], lower[0])
+        cap(capped2[1], rise2[1], 1)
+        for c in quarters:
+            add_share(partial[1], capped1[1], lower[1], c)
+        add_share(result[0], capped1[0], partial[0])
         nc.sync.dma_start(out[:, cols[0]], result[0][:])
-        add_share(result[1], 1, 1, partial[1][:])
+        for c in quarters:
+            add_share(result[1], capped2[1], partial[1], c)
         nc.sync.dma_start(out[:, cols[1]], result[1][:])

@@ -21,7 +21,7 @@ WIDE = 128
 NARROW = 64
 NODES_V = 320
 NODES_V_EARLY = 288
-W_GPSIMD = 56
+W_GPSIMD = 64
 
 
 def tile_picked_huber_none_e_kernel(tc, xT, w1, bound, offs, cen, pos1, pos2, out):
@@ -47,10 +47,10 @@ def tile_picked_huber_none_e_kernel(tc, xT, w1, bound, offs, cen, pos1, pos2, ou
         for j in range(1, PACK):
             nc.sync.dma_start(plane[j][:], x_rows[:, j, :])
         nc.sync.dma_start(w_raw[:], w1.rearrange("(p j) m -> p (j m)", j=PACK))
-        nc.sync.dma_start(b_t[:], bound)
         nc.sync.dma_start(cen_t[:], cen)
         nc.sync.dma_start(pos1_t[:], pos1)
         nc.sync.dma_start(pos2_t[:], pos2)
+        nc.sync.dma_start(b_t[:], bound)
 
         ones = sb.tile([P, 1], F32, name="ones")
         halves = sb.tile([P, 1], F32, name="halves")

@@ -19,9 +19,10 @@ PACK = 4
 PER_COL = 16
 WIDE = 128
 NARROW = 64
-NODES_V = 320
+NODES_V = 352
 NODES_V_EARLY = 288
 W_GPSIMD = 64
+LAST = 1
 
 
 def tile_picked_huber_none_e_kernel(tc, xT, w1, bound, offs, cen, pos1, pos2, out):
@@ -44,7 +45,7 @@ def tile_picked_huber_none_e_kernel(tc, xT, w1, bound, offs, cen, pos1, pos2, ou
 
         nc.sync.dma_start(plane[0][:], x_rows[:, 0, :])
         nc.sync.dma_start(offs_t[:], offs)
-        for j in range(1, PACK):
+        for j in (2, 3, LAST):
             nc.sync.dma_start(plane[j][:], x_rows[:, j, :])
         nc.sync.dma_start(w_raw[:], w1.rearrange("(p j) m -> p (j m)", j=PACK))
         nc.sync.dma_start(cen_t[:], cen)
@@ -68,13 +69,12 @@ def tile_picked_huber_none_e_kernel(tc, xT, w1, bound, offs, cen, pos1, pos2, ou
         def place_s(j, first, count):
             nc.scalar.activation(woven[:, first : first + count, j], plane[j][:].indirect(entries(offs_t, first, count)), ACT.Copy)
 
-        for j, split in ((0, NODES_V_EARLY), (1, NODES_V_EARLY), (2, NODES_V)):
+        for j, split in ((0, NODES_V), (2, NODES_V_EARLY), (3, NODES_V_EARLY)):
             place_v(j, 0, split)
             place_s(j, split, S - split)
-        place_v(PACK - 1, 0, WIDE)
-        place_v(PACK - 1, WIDE, NODES_V - WIDE)
-        place_s(PACK - 1, NODES_V, WIDE)
-        place_s(PACK - 1, NODES_V + WIDE, NARROW)
+        place_v(LAST, 0, WIDE)
+        place_v(LAST, WIDE, NODES_V - WIDE)
+        place_s(LAST, NODES_V, S - NODES_V)
 
         w_woven = sb.tile([P, N, PACK], BF16, name="w_woven", align_bytes=64)
         w_codes = sb.tile([P, N], U32, name="w_codes", align_bytes=64)
@@ -90,7 +90,7 @@ def tile_picked_huber_none_e_kernel(tc, xT, w1, bound, offs, cen, pos1, pos2, ou
         nc.vector.quantize_mx(out=w_codes[:].bitcast(FP8X4), scales=w_scales[:], in_=w_woven[:].rearrange("p m j -> p (m j)"))
 
         y = sb.tile([P, S], F32, name="y")
-        groups = [(NODES_V, WIDE), (0, WIDE), (WIDE, WIDE), (2 * WIDE, NARROW), (NODES_V + WIDE, NARROW)]
+        groups = [(S - WIDE, WIDE), (0, WIDE), (WIDE, WIDE), (2 * WIDE, NARROW), (2 * WIDE + NARROW, NARROW)]
         for g, (first, width) in enumerate(groups):
             source = woven[:, first : first + width, :]
             if g == 0:

@@ -116,46 +116,41 @@ def tile_picked_huber_none_e_kernel(tc, xT, w1, bound, offs, cen, pos1, pos2, ou
 
         half = V // 2
         cols = [slice(0, half), slice(half, V)]
+        quarters = [slice(0, half // 2), slice(half // 2, half)]
 
-        def tiles(name):
-            return [sb.tile([P, half], F32, name=f"{name}{h}") for h in range(2)]
-
-        lower, near1, rise1, rise2, capped1, capped2, partial, result = [
-            tiles(n) for n in ("lower", "near1", "rise1", "rise2", "capped1", "capped2", "partial", "result")
-        ]
-        near2_b = sb.tile([P, half], F32, name="near2_b")
+        def tiles(*names):
+            return [sb.tile([P, half], F32, name=n) for n in names]
 
         def looked_up(lst, h):
             return y[:].indirect(entries(lst, h * half, half))
 
-        for h in range(2):
-            nc.vector.tensor_tensor(lower[h][:], looked_up(cen_t, h), b_t[:, cols[h]], ALU.subtract)
-            nc.scalar.activation(near1[h][:], looked_up(pos1_t, h), ACT.Copy, scale=halves[:])
+        lower_a, near_a, rise1, rise2, capped1, capped2, partial, result_a = tiles(
+            "lower_a", "near_a", "rise1", "rise2", "capped1", "capped2", "partial", "result_a"
+        )
+        lower_b, upper_b, near1_b, near2_b, raised1, raised2, clamped1, clamped2, result_b = tiles(
+            "lower_b", "upper_b", "near1_b", "near2_b", "raised1", "raised2", "clamped1", "clamped2", "result_b"
+        )
+
+        nc.vector.tensor_tensor(lower_a[:], looked_up(cen_t, 0), b_t[:, cols[0]], ALU.subtract)
+        nc.scalar.activation(near_a[:], looked_up(pos1_t, 0), ACT.Copy, scale=halves[:])
+        nc.vector.tensor_tensor(lower_b[:], looked_up(cen_t, 1), b_t[:, cols[1]], ALU.subtract)
+        nc.scalar.activation(near1_b[:], looked_up(pos1_t, 1), ACT.Copy, scale=halves[:])
         nc.scalar.activation(near2_b[:], looked_up(pos2_t, 1), ACT.Copy, scale=halves[:])
-        nc.vector.tensor_tensor(rise2[0][:], looked_up(pos2_t, 0), lower[0][:], ALU.subtract)
+        nc.vector.tensor_tensor(rise2[:], looked_up(pos2_t, 0), lower_a[:], ALU.subtract)
 
-        def lift(dst, near, h):
-            nc.vector.scalar_tensor_tensor(dst[:], lower[h][:], -0.5, near[:], ALU.mult, ALU.add)
-
-        def cap(dst, rise, h, factor=1.0):
-            nc.vector.scalar_tensor_tensor(dst[:], rise[:], factor, b_t[:, cols[h]], ALU.mult, ALU.min)
-
-        def add_share(dst, capped, base, c=slice(0, half)):
-            nc.vector.scalar_tensor_tensor(dst[:, c], capped[:, c], 0.0, base[:, c], ALU.max, ALU.add)
-
-        quarters = [slice(0, half // 2), slice(half // 2, half)]
-        lift(rise1[0], near1[0], 0)
-        lift(rise1[1], near1[1], 1)
-        cap(capped2[0], rise2[0], 0, 0.5)
-        cap(capped1[0], rise1[0], 0)
-        lift(rise2[1], near2_b, 1)
-        cap(capped1[1], rise1[1], 1)
-        add_share(partial[0], capped2[0], lower[0])
-        cap(capped2[1], rise2[1], 1)
+        stt = nc.vector.scalar_tensor_tensor
+        stt(rise1[:], lower_a[:], -0.5, near_a[:], ALU.mult, ALU.add)
+        stt(upper_b[:], b_t[:, cols[1]], 2.0, lower_b[:], ALU.mult, ALU.add)
+        stt(capped2[:], rise2[:], 0.5, b_t[:, cols[0]], ALU.mult, ALU.min)
+        stt(raised1[:], lower_b[:], 0.5, near1_b[:], ALU.mult, ALU.max)
+        stt(capped1[:], rise1[:], 1.0, b_t[:, cols[0]], ALU.mult, ALU.min)
+        stt(raised2[:], lower_b[:], 0.5, near2_b[:], ALU.mult, ALU.max)
+        stt(partial[:], capped2[:], 0.0, lower_a[:], ALU.max, ALU.add)
+        stt(clamped1[:], upper_b[:], 0.5, raised1[:], ALU.mult, ALU.min)
         for c in quarters:
-            add_share(partial[1], capped1[1], lower[1], c)
-        add_share(result[0], capped1[0], partial[0])
-        nc.sync.dma_start(out[:, cols[0]], result[0][:])
+            stt(clamped2[:, c], upper_b[:, c], 0.5, raised2[:, c], ALU.mult, ALU.min)
+        stt(result_a[:], capped1[:], 0.0, partial[:], ALU.max, ALU.add)
+        nc.sync.dma_start(out[:, cols[0]], result_a[:])
         for c in quarters:
-            add_share(result[1], capped2[1], partial[1], c)
-        nc.sync.dma_start(out[:, cols[1]], result[1][:])
+            nc.vector.tensor_tensor(result_b[:, c], clamped1[:, c], clamped2[:, c], ALU.add)
+        nc.sync.dma_start(out[:, cols[1]], result_b[:])

@@ -21,7 +21,7 @@ WIDE = 128
 NARROW = 64
 NODES_V = 352
 NODES_V_EARLY = 288
-W_GPSIMD = 64
+W_GPSIMD = 56
 LAST = 1
 
 

@@ -84,8 +84,8 @@ def tile_picked_huber_none_e_kernel(tc, xT, w1, bound, offs, cen, pos1, pos2, ou
             w_woven[:, 0:W_GPSIMD, :], w_rows[:, :, 0:W_GPSIMD].rearrange("p j m -> p m j"), 1.0, 0.0, ALU.mult, ALU.add
         )
         nc.scalar.copy(
-            w_woven[:, W_GPSIMD:N, :].rearrange("p (c i) j -> p c j i", i=4),
-            w_rows[:, :, W_GPSIMD:N].rearrange("p j (c i) -> p c j i", i=4),
+            w_woven[:, W_GPSIMD:N, :].rearrange("p (c i) j -> p c j i", i=2),
+            w_rows[:, :, W_GPSIMD:N].rearrange("p j (c i) -> p c j i", i=2),
         )
         nc.vector.quantize_mx(out=w_codes[:].bitcast(FP8X4), scales=w_scales[:], in_=w_woven[:].rearrange("p m j -> p (m j)"))
 

from contextlib import ExitStack

import concourse.mybir as mybir

K, T, S, V, N = 512, 1024, 512, 256, 128
FLOPS = 2 * K * N * S

F32 = mybir.dt.float32
BF16 = mybir.dt.bfloat16
U32 = mybir.dt.uint32
U16 = mybir.dt.uint16
U8 = mybir.dt.uint8
FP8X4 = mybir.dt.float8_e4m3fn_x4
ALU = mybir.AluOpType
ACT = mybir.ActivationFunctionType

P = 128
PACK = 4
PER_COL = 16
WIDE = 128
NARROW = 64
NODES_V = 352
NODES_V_EARLY = 288
W_GPSIMD = 56
LAST = 1


def tile_picked_huber_none_e_kernel(tc, xT, w1, bound, offs, cen, pos1, pos2, out):
    nc = tc.nc
    with ExitStack() as ctx:
        lists = ctx.enter_context(tc.tile_pool(name="lists", bufs=1))
        sb = ctx.enter_context(tc.tile_pool(name="sb", bufs=1))
        reuse = ctx.enter_context(tc.tile_pool(name="reuse", bufs=1))
        ps = ctx.enter_context(tc.psum_pool(name="ps", bufs=1))

        offs_t = lists.tile([P, S // PER_COL], U16, name="offs_t")
        cen_t = lists.tile([P, V // PER_COL], U16, name="cen_t")
        pos1_t = lists.tile([P, V // PER_COL], U16, name="pos1_t")
        pos2_t = lists.tile([P, V // PER_COL], U16, name="pos2_t")

        x_rows = xT.rearrange("(p j) t -> p j t", j=PACK)
        plane = [sb.tile([P, T], F32, name=f"plane{j}", align_bytes=256) for j in range(PACK)]
        w_raw = reuse.tile([P, PACK * N], F32, name="w_raw", align_bytes=256, offset=0)
        b_t = sb.tile([P, V], F32, name="b_t", align_bytes=256)

        nc.sync.dma_start(plane[0][:], x_rows[:, 0, :])
        nc.sync.dma_start(offs_t[:], offs)
        for j in (2, 3, LAST):
            nc.sync.dma_start(plane[j][:], x_rows[:, j, :])
        nc.sync.dma_start(w_raw[:], w1.rearrange("(p j) m -> p (j m)", j=PACK))
        nc.sync.dma_start(cen_t[:], cen)
        nc.sync.dma_start(pos1_t[:], pos1)
        nc.sync.dma_start(pos2_t[:], pos2)
        nc.sync.dma_start(b_t[:], bound)

        ones = sb.tile([P, 1], F32, name="ones")
        halves = sb.tile([P, 1], F32, name="halves")
        nc.vector.memset(ones[:], 1.0)
        nc.scalar.activation(halves[:], ones[:], ACT.Copy, scale=0.5)

        def entries(lst, first, count):
            return lst[:, first // PER_COL : (first + count) // PER_COL]

        woven = sb.tile([P, S, PACK], BF16, name="woven", align_bytes=64)

        def place_v(j, first, count):
            nc.vector.tensor_copy(woven[:, first : first + count, j], plane[j][:].indirect(entries(offs_t, first, count)))

        def place_s(j, first, count):
            nc.scalar.activation(woven[:, first : first + count, j], plane[j][:].indirect(entries(offs_t, first, count)), ACT.Copy)

        for j, split in ((0, NODES_V), (2, NODES_V_EARLY), (3, NODES_V_EARLY)):
            place_v(j, 0, split)
            place_s(j, split, S - split)
        place_v(LAST, 0, WIDE)
        place_v(LAST, WIDE, NODES_V - WIDE)
        place_s(LAST, NODES_V, S - NODES_V)

        w_woven = sb.tile([P, N, PACK], BF16, name="w_woven", align_bytes=64)
        w_codes = sb.tile([P, N], U32, name="w_codes", align_bytes=64)
        w_scales = sb.tile([P, N], U8, name="w_scales", align_bytes=64)
        w_rows = w_raw[:].rearrange("p (j m) -> p j m", j=PACK)
        nc.gpsimd.tensor_scalar(
            w_woven[:, 0:W_GPSIMD, :], w_rows[:, :, 0:W_GPSIMD].rearrange("p j m -> p m j"), 1.0, 0.0, ALU.mult, ALU.add
        )
        nc.scalar.copy(
            w_woven[:, W_GPSIMD:N, :].rearrange("p (c i) j -> p c j i", i=2),
            w_rows[:, :, W_GPSIMD:N].rearrange("p j (c i) -> p c j i", i=2),
        )
        nc.vector.quantize_mx(out=w_codes[:].bitcast(FP8X4), scales=w_scales[:], in_=w_woven[:].rearrange("p m j -> p (m j)"))

        y = sb.tile([P, S], F32, name="y")
        groups = [(S - WIDE, WIDE), (0, WIDE), (WIDE, WIDE), (2 * WIDE, NARROW), (2 * WIDE + NARROW, NARROW)]
        for g, (first, width) in enumerate(groups):
            source = woven[:, first : first + width, :]
            if g == 0:
                codes = sb.tile([P, width], U32, name=f"codes{g}", align_bytes=64)
            else:
                codes = reuse.tile([P, width], U32, name=f"codes{g}", align_bytes=256, offset=4 * first)
            scales = sb.tile([P, width], U8, name=f"scales{g}", align_bytes=64)
            nc.vector.quantize_mx(out=codes[:].bitcast(FP8X4), scales=scales[:], in_=source.rearrange("p n j -> p (n j)"))
            acc = ps.tile([P, width], F32, name=f"acc{g}", tag=f"bank{g}")
            nc.tensor.matmul_mx(
                out=acc[:],
                lhsT=w_codes[:].bitcast(FP8X4),
                lhsT_scale=w_scales[:],
                rhs=codes[:].bitcast(FP8X4),
                rhs_scale=scales[:],
                start=True,
                stop=True,
            )
            if g == len(groups) - 2:
                nc.vector.tensor_copy(y[:, first : first + width], acc[:])
            else:
                nc.scalar.copy(y[:, first : first + width], acc[:])

        half = V // 2
        cols = [slice(0, half), slice(half, V)]
        quarters = [slice(0, half // 2), slice(half // 2, half)]

        def tiles(*names):
            return [sb.tile([P, half], F32, name=n) for n in names]

        def looked_up(lst, h):
            return y[:].indirect(entries(lst, h * half, half))

        lower_a, near_a, rise1, rise2, capped1, capped2, partial, result_a = tiles(
            "lower_a", "near_a", "rise1", "rise2", "capped1", "capped2", "partial", "result_a"
        )
        lower_b, upper_b, near1_b, near2_b, raised1, raised2, clamped1, clamped2, result_b = tiles(
            "lower_b", "upper_b", "near1_b", "near2_b", "raised1", "raised2", "clamped1", "clamped2", "result_b"
        )

        nc.vector.tensor_tensor(lower_a[:], looked_up(cen_t, 0), b_t[:, cols[0]], ALU.subtract)
        nc.scalar.activation(near_a[:], looked_up(pos1_t, 0), ACT.Copy, scale=halves[:])
        nc.vector.tensor_tensor(lower_b[:], looked_up(cen_t, 1), b_t[:, cols[1]], ALU.subtract)
        nc.scalar.activation(near1_b[:], looked_up(pos1_t, 1), ACT.Copy, scale=halves[:])
        nc.scalar.activation(near2_b[:], looked_up(pos2_t, 1), ACT.Copy, scale=halves[:])
        nc.vector.tensor_tensor(rise2[:], looked_up(pos2_t, 0), lower_a[:], ALU.subtract)

        stt = nc.vector.scalar_tensor_tensor
        stt(rise1[:], lower_a[:], -0.5, near_a[:], ALU.mult, ALU.add)
        stt(upper_b[:], b_t[:, cols[1]], 2.0, lower_b[:], ALU.mult, ALU.add)
        stt(capped2[:], rise2[:], 0.5, b_t[:, cols[0]], ALU.mult, ALU.min)
        stt(raised1[:], lower_b[:], 0.5, near1_b[:], ALU.mult, ALU.max)
        stt(capped1[:], rise1[:], 1.0, b_t[:, cols[0]], ALU.mult, ALU.min)
        stt(raised2[:], lower_b[:], 0.5, near2_b[:], ALU.mult, ALU.max)
        stt(partial[:], capped2[:], 0.0, lower_a[:], ALU.max, ALU.add)
        stt(clamped1[:], upper_b[:], 0.5, raised1[:], ALU.mult, ALU.min)
        for c in quarters:
            stt(clamped2[:, c], upper_b[:, c], 0.5, raised2[:, c], ALU.mult, ALU.min)
        stt(result_a[:], capped1[:], 0.0, partial[:], ALU.max, ALU.add)
        nc.sync.dma_start(out[:, cols[0]], result_a[:])
        for c in quarters:
            nc.vector.tensor_tensor(result_b[:, c], clamped1[:, c], clamped2[:, c], ALU.add)
        nc.sync.dma_start(out[:, cols[1]], result_b[:])
